import numpy as np, ml_dtypes
CORES = [25,29,65,69,153,157,193,197]
N = 8
import mx_ref
BF = ml_dtypes.bfloat16
def gcols(t, e):
    v = np.concatenate([t.reshape(8, 16, -1, 4), np.zeros((8, 16, 1, 4), BF)], axis=2)
    return np.ascontiguousarray(np.stack([v[g][:, e[g]] for g in range(8)])).reshape(128, -1)
def tile(rs):
    return np.stack(rs, axis=2).reshape(128, -1).astype(BF)
def pick(q, e):
    c = np.concatenate([q[0].reshape(128, -1, 4), np.zeros((128, 1, 4), np.uint8)], axis=1); s = np.concatenate([q[1], np.ones((16, 1), np.uint8)], axis=1)
    return (np.ascontiguousarray(c[:, e].reshape(128, -1)), np.ascontiguousarray(s[:, e]))
def join(*qs):
    return (np.concatenate([q[0] for q in qs], axis=1), np.concatenate([q[1] for q in qs], axis=1))
def put(q, e, v):
    c, s = q[0].reshape(128, -1, 4).copy(), q[1].copy(); c[:, e] = v[0].reshape(128, -1, 4); s[:, e] = v[1]
    return (c.reshape(128, -1), s)
def pk(c, s):
    return (np.ascontiguousarray(c), mx_ref.live(s))
def emit(q):
    return q[0], q[1]
def packed(v, rng):
    q = [mx_ref.quantize(np.ascontiguousarray(v[r])) for r in range(N)]
    return np.stack([a for a, b in q]), np.stack([mx_ref.plane(b, rng) for a, b in q])
def values_of_codes():
    e, c = np.zeros((128, 128, 4), np.float32), np.zeros((128, 2, 4), np.uint8)
    e[np.arange(128), np.arange(128), 0] = 1
    c[:127, :, 0] = np.arange(256).reshape(2, 128).T[:127]
    return mx_ref.matmul(mx_ref.quantize(e.reshape(128, 512).astype(BF)), (c.reshape(128, 8), np.full((16, 2), 127, np.uint8))).T.reshape(-1).astype(np.float64)
CODE_VALUE, SCALE_VALUE = values_of_codes(), 2.0 ** (np.arange(256) - 127.0)
def decode(q):
    return (CODE_VALUE[q[0]].reshape(16, 8, -1, 4) * SCALE_VALUE[q[1]][:, None, :, None] + 0.0).reshape(128, -1).astype(np.float32)
def f(rng, *shape):
    return mx_ref.flush((rng.standard_normal(shape, dtype=np.float32) * np.exp2(rng.integers(-2, 3, shape[:-1] + (1,)))).astype(BF))
def wide(rng, *shape, cols=0):
    v = rng.standard_normal(shape, dtype=np.float32) * np.exp2(rng.integers(-12, 13, shape)).astype(np.float32)
    if cols: v *= np.repeat(np.exp2(rng.integers(-cols, cols + 1, shape[:-2] + (1, shape[-1] // 4))) * (rng.random(shape[:-2] + (1, shape[-1] // 4)) > 0.0625), 4, axis=-1).astype(np.float32)
    return mx_ref.flush(v.astype(BF))
J, K, R = 10, 4, 3
def cycle(t, o):
    i = np.arange(len(t))
    a, b = o[:, 0], o[:, 1]
    c = np.where(t[i, a, b] == o[:, 2], o[:, 3], o[:, 2])
    m = np.zeros((len(t), 16), bool)
    for k in range(6):
        m[i, c] = True
        c = t[i, a, c]
        m[i, c] = True
        c = t[i, b, c]
    return m
def switched(t, o):
    i = np.arange(len(t))
    a, b = o[:, 0], o[:, 1]
    m = cycle(t, o)
    inside = m[:, :, None] & m[:, None, :]
    aa, bb = a[:, None, None], b[:, None, None]
    new = np.where(inside & (t == aa), bb, np.where(inside & (t == bb), aa, t))
    ra, rb = np.where(m, t[i, b], t[i, a]), np.where(m, t[i, a], t[i, b])
    new[i, a] = ra
    new[i, :, a] = ra
    new[i, b] = rb
    new[i, :, b] = rb
    return new
def numbered(e):
    return (e.reshape(N, 8, 16, J).transpose(0, 1, 3, 2) + 16 * np.arange(16)).reshape(N, 8, 16 * J)
FIELD = (((np.arange(16) + 1) % 16)[:, None] ^ ((np.arange(16) + 1) % 16)[None, :]) + 15
FIELD = FIELD % 16
def orders(rng, n):
    return np.argsort(rng.random((n, 15)), axis=1)
def renamed(rng, t):
    n = len(t)
    s = np.concatenate([orders(rng, n), np.full((n, 1), 15)], axis=1)
    k = np.argsort(s, axis=1)
    i = np.arange(n)[:, None, None]
    return s[i, t[i, k[:, :, None], k[:, None, :]]]
def systems(rng):
    t = renamed(rng, np.stack([FIELD] * (N * 128)))
    for k in range(16): t = switched(t, orders(rng, N * 128))
    return t
def stored(t):
    return t.astype(np.int32).reshape(N, 128, 256)
def big(v):
    v = v.astype(np.float32)
    v[np.abs(v) < np.float32(2.0 ** -16)] = 0
    return v.astype(BF)
def odd(rng):
    s = (N, 8, 8, 16, 16, 4)
    k = rng.integers(8, 15, s)
    k[:, :, 1, :, :, 0] = 13 + k[:, :, 1, :, :, 0] % 2
    v = (1.0 + (2 * rng.integers(0, 64, s) + 1) * 2.0 ** -7) * 2.0 ** -k.astype(float)
    v[:, :, 0, :, :, 0] = 1.96875
    return (v * (rng.integers(0, 2, s) * 2.0 - 1.0)).astype(np.float32).astype(BF)
def numbers_of(rng):
    return {"x": big(f(rng, N, 128, 1024)), "u": np.array(f(rng, N, 128, 512)), "v": np.array(f(rng, N, 128, 512))}
def weights(rng, still=[]):
    w = big(f(rng, N, 128, 2048)).reshape(N, 8, 16, 4, 8, 16, 4)
    for i in still:
        w[:, :, i] = 0
        w[:, :, :, :, :, i] = 0
    c, p = packed(w.reshape(N, 128, 2048), rng)
    return {"wc": c, "ws": p}
def setup_inputs(rng):
    return {**numbers_of(rng), "tri": stored(systems(rng)), **weights(rng)}
def setup_inputs_ties(rng):
    d = numbers_of(rng)
    x = d["x"].reshape(N, 8, 16, 16, 16, 4)
    k = rng.integers(0, 3, (N, 8, 16, 16)) - 4 * rng.integers(0, 2, (N, 8, 16, 1))
    k = np.where(rng.random((N, 8, 16, 1)) < 0.25, k[:, :, :, :1], k)
    x[:, :, 0] = 0
    x[:, :, 0, :, :, 0] = k.astype(np.float32).astype(BF)
    x[:, :, 8:] = odd(rng)
    u = d["u"].reshape(N, 128, 128, 4)
    u[:, :, ::16] = 0
    o = rng.permutation(N)
    for r in range(N):
        e = 16 * rng.permutation(8)[:2]
        for h in range(0, 128, 16): u[r, h + 9 if h in e else h, h, 0] = 0.0 if r == o[0] else -1.0 if r == o[1] else 1.0
    return {"x": x.reshape(N, 128, 1024), "u": u.reshape(N, 128, 512), "v": d["v"], "tri": stored(systems(rng)), **weights(rng, [0])}
def setup_inputs_near(rng):
    d = numbers_of(rng)
    x = d["x"].astype(np.float32).reshape(N, 8, 16, 16, 16, 4)
    x[:, :, 0] = 0
    x[:, :, 8:] = 0
    x[:, :, 0, :, :, 0] = rng.integers(0, 2, (N, 8, 16, 1)) * 2.0 - 1.0
    s = rng.integers(0, 16, (N, 8, 16, 16))
    x[:, :, 8] = ((s[..., None] >> np.arange(4)) & 1) * np.exp2(np.arange(4) - 23.0)
    u = d["u"].reshape(N, 128, 128, 4)
    u[:, :, ::16] = 0
    o = rng.permutation(N) % 4
    for r in range(N):
        k = 1.0 if o[r] == 0 else 2.0 ** -30
        if o[r] < 2: x[r, :, 11, :, :, 0] = 2.0 ** -10
        if o[r] == 2:
            a = np.zeros((8, 16, 16), np.float32)
            e = np.argsort(rng.random((8, 16, 15)), axis=2)
            np.put_along_axis(a, e[:, :, :1], 1.0, axis=2)
            np.put_along_axis(a, e[:, :, 1:2], -1.0, axis=2)
            x[r, :, 0, :, :, 0] = a
        if o[r] == 3:
            x[r, :, 8] = 0
            x[r, :, 10, :, :, 0] = rng.integers(-7, 8, (8, 16, 16)) * 2.0 ** -27
        for h in range(0, 128, 16):
            if o[r] < 2:
                u[r, h, h, 0] = k
                u[r, h + 11, h, 0] = k
            if o[r] == 2: u[r, h, h, 0] = 1.0
            if o[r] < 3: u[r, h + 8, h] = k
            else: u[r, h + 10, h, 0] = k
    return {"x": x.reshape(N, 128, 1024).astype(BF), "u": u.reshape(N, 128, 512), "v": d["v"], "tri": stored(systems(rng)), **weights(rng, [0, 8, 9, 10, 11, 12, 13, 14, 15])}
def setup_inputs_late(rng):
    d = numbers_of(rng)
    n = N * 128
    o = rng.permutation(N)
    t = systems(rng)
    for r in o[:N // 2]: t[128 * r:128 * r + 128] = renamed(rng, np.stack([FIELD] * 128))
    best = orders(rng, n)
    most = np.count_nonzero(cycle(t, best), axis=1)
    for j in range(60):
        e = orders(rng, n)
        m = np.count_nonzero(cycle(t, e), axis=1)
        best[m > most] = e[m > most]
        most = np.maximum(most, m)
    i = np.arange(n)
    third = t[i, best[:, 0], best[:, 1]]
    c = np.where(third == best[:, 2], best[:, 3], best[:, 2])
    k = np.argsort(best, axis=1).astype(float)
    k[i, c] = 1.6
    k[i[::2], third[::2]] = 1.3
    p = np.argsort(np.argsort(k, axis=1), axis=1).reshape(N, 8, 16, 15)
    s = 15.0 - p
    s[o[::2]] -= 16.0
    x = d["x"].reshape(N, 8, 16, 16, 16, 4)
    x[:, :, 0, :, :15, 0] = s.astype(np.float32).astype(BF)
    x[:, :, 8:] = odd(rng)
    u = d["u"].reshape(N, 128, 128, 4)
    u[:, :, ::16] = 0
    for h in range(0, 128, 16): u[:, h, h, 0] = 1
    return {"x": x.reshape(N, 128, 1024), "u": u.reshape(N, 128, 512), "v": d["v"], "tri": stored(t), **weights(rng)}
def setup_inputs_huge(rng):
    d = numbers_of(rng)
    q = int(rng.integers(N))
    c = rng.integers(0, 2, (N, 1, 1, 16, 16, 1)) * 2.0 - 1.0
    c[:, :, :, ::2] = c[:, :, :, ::2, :1]
    x = (0.6 + 0.06 * rng.random((N, 8, 1, 16, 16, 1)) + 0.03 * rng.random((N, 8, 16, 16, 16, 4))) * c
    s = -np.ones((16, 16))
    np.put_along_axis(s, np.argsort(rng.random((16, 15)), axis=1)[:, :3], 1.0, axis=1)
    x[q] = 0.875 * s[None, None, :, :, None]
    h = rng.integers(0, 8, (1, 16, 16, 1))
    x[q, 0, :2] *= np.where(4 * np.arange(2)[:, None, None, None] + np.arange(4) < h, 0.5, 1.0)
    a = 2.0 ** 29 * (1.0 - 0.1 * rng.random((N, 8, 16, 8, 4)))
    for g in range(8): a[:, g, :, g] *= 2.0
    a *= rng.integers(0, 2, (N, 1, 1, 8, 1)) * 2.0 - 1.0
    a[q] = 2.0 ** 30
    u = d["u"].reshape(N, 128, 128, 4)
    u[:, :, ::16] = a.reshape(N, 128, 8, 4).astype(np.float32).astype(BF)
    w = np.zeros((N, 128, 4, 128, 4), np.float32)
    i = np.arange(128)
    for b in range(4): w[:, i, b, i, b] = -1
    wc, ws = packed(w.reshape(N, 128, 2048).astype(BF), rng)
    return {"x": (2.0 ** 30 * x).astype(np.float32).reshape(N, 128, 1024).astype(BF), "u": u.reshape(N, 128, 512), "v": d["v"], "tri": stored(systems(rng)), "wc": wc, "ws": ws}
def setup_inputs_spread(rng):
    d = setup_inputs(rng)
    d["x"] = big(wide(rng, N, 128, 1024, cols=6))
    return d
def check_inputs(d):
    b = []
    for k in ("x", "u", "v"):
        a = np.abs(d[k].astype(np.float32))
        if not (np.isfinite(a).all() and ((a == 0) | (a >= 2.0 ** -30) & (a <= 2.0 ** 30)).all()): b.append("a value of " + k)
    if not ((d["tri"] >= 0) & (d["tri"] <= 15)).all(): b.append("an entry of tri")
    t = np.clip(d["tri"], 0, 15).astype(np.int64).reshape(-1, 16, 16)
    i = np.arange(16)
    if (t != t.transpose(0, 2, 1)).any() or (t[:, i, i] != 15).any() or (t[:, :, 15] != i).any() or (np.take_along_axis(t, t, axis=2) != i).any(): b.append("a table of tri that isn't one of triples")
    none, least, most = [emit(mx_ref.quantize(np.full((128, 16), k, np.float32).astype(BF)))[1][0, 0] for k in (0.0, 2.0 ** -30, 2.0 ** 30)]
    for r in range(N):
        if ((d["wc"][r] & 0x7F) == 0x7F).any(): b.append("wc: a code that is no number")
        s = mx_ref.live(d["ws"][r])
        if ((s != none) & ((s < least) | (s > most))).any(): b.append("ws: a scale out of range")
    return b
def reference(x, u, v, tri, wc, ws):
    qu = [mx_ref.quantize(u[r]) for r in range(N)]
    lay = [pk(wc[r], ws[r]) for r in range(N)]
    now = [x[r] for r in range(N)]
    t = tri.astype(np.int64).reshape(N * 128, 16, 16)
    i = np.arange(N * 128)[:, None]
    for h in range(R):
        q = [mx_ref.quantize(now[r]) for r in range(N)]
        own = [decode(q[r]).astype(BF) for r in range(N)]
        s = np.concatenate([(mx_ref.matmul(qu[r], q[r])[::16] + np.float32(0.0)).reshape(128, 16)[:, :15] for r in range(N)])
        o = np.argsort(-s, axis=1, kind="stable")
        first, second = numbered(o[:, :J]), numbered(o[:, 1:J + 1])
        third = numbered(t[i, o[:, :J], o[:, 1:J + 1]])
        z = [((gcols(own[r], second[r]).astype(np.float32) + gcols(own[r], third[r]).astype(np.float32)) * np.float32(0.5)).astype(BF) for r in range(N)]
        zq = [mx_ref.quantize(z[r]) for r in range(N)]
        for r in range(N):
            w = join(pick(zq[(r - 1) % N], np.arange(16 * K)), pick(zq[r], np.arange(16 * K, 16 * J)))
            made = tile([mx_ref.matmul(pick(lay[r], np.arange(128 * b, 128 * b + 128)), w) * np.float32(0.03125) + z[r][:, b::4].astype(np.float32) for b in range(4)]).reshape(8, 16, 16 * J, 4)
            new = np.array(own[r]).reshape(8, 16, 256, 4)
            for g in range(8): new[g][:, first[r, g]] = made[g]
            now[r] = new.reshape(128, 1024)
        t = switched(t, o)
    y, ot = np.zeros((N, 128, 256), np.float32), t.reshape(N, 128, 256).astype(np.float32)
    oc, osc = np.zeros((N, 128, 1024), np.uint8), np.zeros((N, 16, 256), np.uint8)
    for r in range(N):
        q = mx_ref.quantize(now[r])
        y[r] = mx_ref.matmul(mx_ref.quantize(v[r]), q)
        oc[r], osc[r] = emit(q)
    return {"y": y, "ot": ot, "oc": oc, "osc": osc}

@@ -1,0 +1,409 @@
+from concourse.mybir import dt, AluOpType, ActivationFunctionType
+
+R = 3
+F8, U8, BF, F32, I32, U16 = "float8_e4m3fn_x4", "uint8", "bfloat16", "float32", "int32", "uint16"
+WN = 416
+
+_SB = {
+    BF: dict(xin=1024, uin=512, vin=512, ones=128, ident=128, ebig=528, yi=256, msk=256, keep=272, flip=240, targ=176, m32=512,
+             cm=240, rk=256, nq=176, ob=176, lk=160, ms=160, hf=1024, aa=640, zl=512, ze=512, z32=640, wn=4 * WN, xn=1024,
+             nn=512, rs=512, sg=256, sh=2, zz=768, vs=256, d0=1024, d1=1024, u4=1024, uu=256, tb0=256, tb1=256, tb2=256),
+    F32: dict(pif=1, x2=32, inid=16, rkc=32, mb=240, sc=256, g1=240, o16=32, rr=64, of2=32, oft=32, rin=32, sm=8, kb=16, tw=192,
+              tb3=256, yo=256),
+    I32: dict(tin=256, ia=48, ib=48, ic=32, icol=16, ipart=2, ipm=4),
+    U16: dict(lx=16, lu=16, lcmp=32, linv=16, ltr=16, lhalf=2, osec=16, oidx=16, othird=16, onew=16),
+    F8: dict(wq=512, xq0=256, uq0=128, uq=128, vq=128, eq=512),
+    U8: dict(wp=512, xp0=256, up0=128, up=128, vp=128, ep=512),
+}
+for _h in range(R):
+    _SB[F8].update({"zq%d" % _h: 128, "qw%d" % _h: 192, "rc%d" % _h: 64})
+    _SB[U8].update({"zp%d" % _h: 128, "pw%d" % _h: 192, "rp%d" % _h: 64})
+for _h in range(R + 1):
+    _SB[F8]["xc%d" % _h] = 256
+    _SB[U8]["xs%d" % _h] = 256
+SCRATCH = {_k: ("sbuf", [128, _n], _d) for _d in _SB for _k, _n in _SB[_d].items()}
+SCRATCH["ps"] = ("psum", [128, 4096], F32)
+
+SEMAPHORES = ["cv", "ca", "ct", "cg", "sent"] + ["arr%d" % h for h in range(R)] + ["dm%d" % k for k in range(20)]
+
+A = AluOpType
+AF = ActivationFunctionType
+
+
+def _mask(es):
+    m = 0
+    for e in es:
+        m |= 1 << e
+    return m
+
+
+def _relays(src, dst, group, topo):
+    cs = [c for c in topo.cores_of(src) if c not in group and topo.may_write(c, dst)]
+    return sorted(cs, key=lambda c: (topo.die(c) != topo.die(src), c))[:2]
+
+
+def _emit(g, T, ops):
+    q = {"v": g.vector, "a": g.scalar, "t": g.tensor, "g": g, "s": g.sync}
+    cs = {"v": "cv", "a": "ca", "t": "ct", "g": "cg"}
+    lastw, readers = {}, {}
+    known = {e: ({}, set()) for e in q}
+    snap, waits, sig = [], [], set()
+    for i, o in enumerate(ops):
+        e = o["e"]
+        deps = set()
+        for k in o["r"]:
+            if k in lastw:
+                deps.add(lastw[k])
+        for k in o["w"]:
+            if k in lastw:
+                deps.add(lastw[k])
+            deps.update(readers.get(k, []))
+        w = []
+        if e is not None:
+            kc, ks = known[e]
+            for d in sorted(deps, reverse=True):
+                p = ops[d]
+                if p["sem"] is None:
+                    if kc.get(p["e"], -1) >= d:
+                        continue
+                    kc[p["e"]] = d
+                elif d in ks:
+                    continue
+                else:
+                    ks.add(d)
+                w.append(d)
+                sig.add(d)
+                for k2, v2 in snap[d][0].items():
+                    if kc.get(k2, -1) < v2:
+                        kc[k2] = v2
+                ks.update(snap[d][1])
+            snap.append((dict(kc), set(ks)))
+        else:
+            snap.append(({}, set()))
+        waits.append(w)
+        for k in o["r"]:
+            readers.setdefault(k, []).append(i)
+        for k in o["w"]:
+            lastw[k] = i
+            readers[k] = []
+    cnt, val = {e: 0 for e in cs}, {}
+    for i, o in enumerate(ops):
+        if o["sem"] is None and i in sig:
+            cnt[o["e"]] += 1
+            val[i] = (cs[o["e"]], cnt[o["e"]])
+        elif o["sem"] is not None:
+            val[i] = (o["sem"], o["n"])
+    for i, o in enumerate(ops):
+        if o["e"] is None:
+            continue
+        for d in waits[i]:
+            q[o["e"]].wait_ge(T.sem[val[d][0]], val[d][1])
+        if o["f"] is None:
+            continue
+        ins = o["f"](q[o["e"]])
+        if o["kind"] == "dma":
+            ins.then_inc(T.sem[o["sem"]], 16)
+        elif o["kind"] == "c" and i in sig:
+            ins.then_inc(T.sem[val[i][0]], 1)
+
+
+def _relay_program(g, core, T, topo, dst, part):
+    rid, pid = topo.addr(dst, core)
+    es = topo.engines(core, dst)
+    n_in = len(topo.engines(core, core)) // 2
+    for h in range(R):
+        g.wait_ge(T.sem["arr%d" % h], n_in)
+        if part == 0:
+            o, i = T["qw%d" % h][:, 0:64].bitcast(dt.uint8), T["rc%d" % h][:].bitcast(dt.uint8)
+        else:
+            o, i = T["pw%d" % h][:, 0:64], T["rp%d" % h][:]
+        g.remote_dma(o, i, T.sem["arr%d" % h], T.sem.sent, pid, rid, _mask(es))
+    g.wait_ge(T.sem.sent, R * len(es))
+
+
+def rank_program(g, core, T, topo):
+    cores = list(T.cores)
+    n = len(cores)
+    rank = T.rank_of(core)
+    if rank is None:
+        for r in range(n):
+            s, d = cores[r], cores[(r + 1) % n]
+            if not topo.may_write(s, d):
+                rl = _relays(s, d, cores, topo)
+                if core in rl:
+                    _relay_program(g, core, T, topo, d, rl.index(core))
+        return
+    nxt, prv = cores[(rank + 1) % n], cores[(rank - 1) % n]
+    direct = topo.may_write(core, nxt)
+    to = [nxt, nxt] if direct else _relays(core, nxt, cores, topo)
+    if topo.may_write(prv, core):
+        n_arr = len(topo.engines(prv, core))
+    else:
+        n_arr = sum(len(topo.engines(c, core)) for c in _relays(prv, core, cores, topo))
+
+    ops = []
+    ndma = [0]
+
+    def op(e, f, r=(), w=(), kind="c", sem=None, cnt=0):
+        ops.append({"e": e, "f": f, "r": list(r), "w": list(w), "kind": kind, "sem": sem, "n": cnt})
+
+    def dma(e, out, in_, r=(), w=()):
+        op(e, lambda q: q.dma_start(out, in_), r, w, "dma", "dm%d" % ndma[0], 16)
+        ndma[0] += 1
+
+    def ts(out, in0, s1, s2, o0, o1, r, w):
+        if o1 is None:
+            op("v", lambda q: q.tensor_scalar(out, in0, s1, None, o0), r, w)
+        else:
+            op("v", lambda q: q.tensor_scalar(out, in0, s1, s2, o0, o1), r, w)
+
+    def tt(out, a, b, o, r, w):
+        op("v", lambda q: q.tensor_tensor(out, a, b, o), r, w)
+
+    def scan(out, a, b, r, w):
+        op("v", lambda q: q.tensor_tensor_scan(out, a, b, 0.0, A.mult, A.add), r, w)
+
+    def cp(out, a, r, w):
+        op("v", lambda q: q.tensor_copy(out, a), r, w)
+
+    def fill(ap, c, w):
+        op("v", lambda q: q.memset(ap, c), (), w)
+
+    def act(out, a, r, w, func=AF.Copy, **kw):
+        op("a", lambda q: q.activation(out, a, func, **kw), r, w)
+
+    def quant(c, s, a, r, w):
+        op("v", lambda q: q.quantize_mx(c, s, a), r, w)
+
+    def mm(bank, n_, lc, ls, rc, rs_, r):
+        op("t", lambda q: q.matmul_mx(T.ps[:, 512 * bank:512 * bank + n_], lc, ls, rc, rs_, True, True), r, ["b%d" % bank])
+
+    def iota(out, pat, base, cmul, w, flt=False):
+        if flt:
+            op("g", lambda q: q.iota(out, pat, base, cmul, allow_small_or_imprecise_dtypes=True), (), w)
+        else:
+            op("g", lambda q: q.iota(out, pat, base, cmul), (), w)
+
+    def bank(b, n_):
+        return T.ps[:, 512 * b:512 * b + n_]
+
+    def four(name):
+        return ["%s%d" % (name, b) for b in range(4)]
+
+    u32 = dt.uint32
+    vv, cs, rho = 0, 256, 512
+    dma("s", T.xin[:], T.x[:], (), ["xin"])
+    dma("a", T.uin[:], T.u[:], (), ["uin"])
+    dma("s", T.tin[:], T.tri[:], ["uin"], ["tin"])
+    dma("s", T.wq[:].bitcast(dt.uint8), T.wc[:], ["xin"], ["wq"])
+    dma("s", T.wp[:], T.ws[:], (), ["wp"])
+    fill(T.ones[:], 1.0, ["ones"])
+    iota(T.icol[:], [[16, 16]], 0, 0, ["icol"])
+    op("g", lambda q: q.affine_select(T.ident[:], T.ones[:], [[-1, 128]], A.is_equal, 0.0, 0, 1), ["ones"], ["ident"])
+    iota(T.ia[:, 0:16], [[1, 16]], 0, 16, ["ia0"])
+    iota(T.ipart[:], [[0, 2]], 0, 1, ["ipart"])
+    iota(T.ia[:, 16:32], [[16, 16]], 16, 16, ["ia1"])
+    iota(T.ia[:, 32:48], [[0, 16]], 2303, -16, ["ia2"])
+    iota(T.yi[:], [[0, 16], [1, 16]], 0, 0, ["yi"], True)
+    iota(T.targ[:], [[1, 11], [-1, 16]], 1, 0, ["targ"], True)
+    iota(T.rkc[:, 0:16], [[-1, 16]], 14, 0, ["rkc0"], True)
+    iota(T.m32[:], [[0, 512]], -32, 0, ["m32"], True)
+    iota(T.x2[:], [[0, 2], [1, 16]], 0, 0, ["x2"], True)
+    iota(T.inid[:], [[33, 16]], -512, 0, ["inid"], True)
+    iota(T.rkc[:, 16:32], [[1, 16]], 10, 0, ["rkc1"], True)
+    iota(T.zz[:], [[0, 768]], 0, 0, ["zz", "cs", "rho"], True)
+    iota(T.ze[:, 384:512], [[0, 128]], 0, 0, ["zep"], True)
+    dma("g", T.vin[:], T.v[:], (), ["vin"])
+    fill(T.ebig[:], 0.0, ["ebig"])
+    fill(T.keep[:], 1.0, ["keep"])
+    fill(T.flip[:], 1.0, ["flip"])
+    fill(T.zl[:, 256:512], 0.0, ["zlp"])
+    fill(T.sc[:, 255:256], -1.0e29, ["scp"])
+    fill(T.rk[:, 255:256], 16.0, ["rkp"])
+    fill(T.keep[:, 0:272:16], 0.0, ["keep"])
+    fill(T.flip[:, 0:240:16], 0.0, ["flip"])
+    cp(T.ebig[:, 3:515:4], T.ident[:], ["ident"], ["ebig"])
+    fill(T.flip[:, 15:240:15], -1.0, ["flip"])
+    cp(T.lu[:], T.icol[:], ["icol"], ["lu"])
+    ts(T.ib[:, 0:16], T.ia[:, 0:16], 255, None, A.bitwise_and, None, ["ia0"], ["ib0"])
+    for b in range(4):
+        quant(T.eq[:, 128 * b:128 * b + 128], T.ep[:, 128 * b:128 * b + 128], T.ebig[:, 3 - b:515 - b], ["ebig"], ["e%d" % b])
+    cp(T.lx[:], T.ib[:, 0:16], ["ib0"], ["lx"])
+    ts(T.ipm[:, 0:2], T.ipart[:], 15, None, A.bitwise_and, None, ["ipart"], ["ipm0"])
+    ts(T.ib[:, 16:48], T.ia[:, 16:48], 255, None, A.bitwise_and, None, ["ia1", "ia2"], ["ib1"])
+    cp(T.pif[:], T.ipm[:, 0:1], ["ipm0"], ["pif"])
+    quant(T.uq0[:], T.up0[:], T.uin[:], ["uin"], ["uq0"])
+    tt(T.ic[:, 0:16], T.ib[:, 16:32], T.icol[:], A.min, ["ib1", "icol"], ["ic0"])
+    cp(T.uq[:].bitcast(u32), T.uq0[:].bitcast(u32).indirect(T.lu[:, 0:8]), ["uq0", "lu"], ["uq"])
+    act(T.up[:], T.up0[:].indirect(T.lu[:, 0:8]), ["uq0", "lu"], ["up"])
+    quant(T.xq0[:], T.xp0[:], T.xin[:], ["xin"], ["xq0"])
+    tt(T.ic[:, 16:32], T.ib[:, 16:32], T.icol[:], A.max, ["ib1", "icol"], ["ic1"])
+    for k in range(2):
+        cp(T.xc0[:, 128 * k:128 * k + 128].bitcast(u32), T.xq0[:].bitcast(u32).indirect(T.lx[:, 8 * k:8 * k + 8]), ["xq0", "lx"], ["xc0%d" % k])
+        act(T.xs0[:, 128 * k:128 * k + 128], T.xp0[:].indirect(T.lx[:, 8 * k:8 * k + 8]), ["xq0", "lx"], ["xs0%d" % k])
+    ts(T.msk[:], T.yi[:], T.pif[:], None, A.is_equal, None, ["yi", "pif"], ["msk"])
+
+    def o_(j):
+        return T.ob[:, 16 * j + 15:16 * j + 16]
+
+    def plane(b):
+        return T.hf[:, 256 * b:256 * b + 256]
+
+    for h in range(R):
+        xc, xs = T["xc%d" % h], T["xs%d" % h]
+        kx = [["xc%d%d" % (h, k), "xs%d%d" % (h, k)] for k in range(2)]
+        tb, tn = T["tb%d" % h], T["tb%d" % (h + 1)]
+        ktb = "tb%d" % h
+        zq, zp, qw, pw = T["zq%d" % h], T["zp%d" % h], T["qw%d" % h], T["pw%d" % h]
+        for k in range(2):
+            mm(k, 128, T.uq[:], T.up[:], xc[:, 128 * k:128 * k + 128], xs[:, 128 * k:128 * k + 128], ["uq", "up"] + kx[k])
+        for b in range(4):
+            mm(2 + b, 256, T.eq[:, 128 * b:128 * b + 128], T.ep[:, 128 * b:128 * b + 128], xc[:], xs[:], ["e%d" % b] + kx[0] + kx[1])
+        tt(T.mb[:, 0:128], bank(0, 128), T.msk[:, 0:128], A.mult, ["msk"], ["mb0", "b0"])
+        tt(T.mb[:, 128:240], bank(1, 112), T.msk[:, 128:240], A.mult, ["msk"], ["mb1", "b1"])
+        if h == 0:
+            ts(T.lcmp[:], T.ic[:], 15.0, None, A.add, None, ["ic0", "ic1"], ["lcmp"])
+        else:
+            act(T.d1[:, 3:1024:4], tb[:], [ktb], ["d13"], scale=0.5)
+        act(plane(0), bank(2, 256), (), ["hf0", "b2"], scale=0.5)
+        scan(T.sc[:, 0:240], T.keep[:, 0:240], T.mb[:], ["keep", "mb0", "mb1"], ["sc"])
+        if h == 0:
+            cp(T.linv[:], T.ib[:, 32:48], ["ib1"], ["linv"])
+        cp(T.g1[:, 0:128], T.sc[:].indirect(T.lcmp[:, 16:24]), ["sc", "scp", "lcmp"], ["g1a"])
+        act(T.g1[:, 128:240], T.sc[:].indirect(T.lcmp[:, 24:31]), ["sc", "scp", "lcmp"], ["g1b"])
+        tt(T.cm[:], T.sc[:].indirect(T.lcmp[:, 0:15]), T.g1[:], A.is_ge, ["sc", "scp", "lcmp", "g1a", "g1b"], ["cm"])
+        for b in range(1, 4):
+            act(plane(b), bank(2 + b, 256), (), ["hf%d" % b, "b%d" % (2 + b)], scale=0.5)
+        for b in range(2):
+            act(T.wn[:, WN * b + 160:WN * b + WN], plane(b), ["hf%d" % b], ["wg%d" % b], scale=64.0)
+        if h == 0:
+            cp(T.tb0[:], T.tin[:], ["tin"], ["tb0"])
+        scan(T.rk[:, 0:240], T.flip[:], T.cm[:], ["flip", "cm"], ["rk"])
+        tt(T.nq[:], T.rk[:].indirect(T.linv[:, 0:11]), T.targ[:], A.not_equal, ["rk", "rkp", "linv", "targ"], ["nq"])
+        tt(T.rr[:, 0:16], T.rk[:, 15:256:16], T.rkc[:, 0:16], A.add, ["rk", "rkp", "rkc0"], ["rr0"])
+        scan(T.ob[:], T.nq[:], T.keep[:, 1:177], ["nq", "keep"], ["ob"])
+        tt(T.sg[:, 15:256:16], T.nq[:, 16:32], T.nq[:, 0:16], A.subtract, ["nq"], ["sg"])
+        ts(T.osec[:, 0:10], T.ob[:, 31:176:16], 16.0, T.pif[:], A.mult, A.add, ["ob", "pif"], ["osec"])
+        ts(T.o16[:, 0:10], T.ob[:, 15:160:16], 16.0, None, A.mult, None, ["ob"], ["o16"])
+        for b in range(4):
+            act(T.aa[:, 160 * b:160 * b + 64], plane(b).indirect(T.osec[:, 0:4]), ["hf%d" % b, "osec"], ["aa0%d" % b])
+        for b in range(4):
+            act(T.aa[:, 160 * b + 64:160 * b + 160], plane(b).indirect(T.osec[:, 4:10]), ["hf%d" % b, "osec"], ["aa1%d" % b])
+        ts(T.nn[:, 0:256], tb[:], o_(0), None, A.not_equal, None, [ktb, "ob"], ["nn0"])
+        tt(T.o16[:, 16:26], T.o16[:, 0:10], T.ob[:, 31:176:16], A.add, ["ob", "o16"], ["o17"])
+        ts(T.nn[:, 256:512], tb[:], o_(1), None, A.not_equal, None, [ktb, "ob"], ["nn1"])
+        cp(T.oidx[:, 0:10], T.o16[:, 16:26], ["o17"], ["oidx"])
+        ts(T.sh[:, 0:1], o_(3), o_(2), -32.0, A.subtract, A.mult, ["ob"], ["sm0"])
+        tt(T.lk[:], tb[:].indirect(T.oidx[:, 0:10]), T.msk[:, 0:160], A.mult, [ktb, "msk", "oidx"], ["lk"])
+        scan(T.rs[:], T.nn[:], T.m32[:], ["nn0", "nn1", "m32"], ["rs"])
+        scan(T.ms[:], T.keep[:, 0:160], T.lk[:], ["keep", "lk"], ["ms"])
+        ts(T.sm[:, 1:2], o_(2), -32.0, 512.0, A.mult, A.add, ["ob"], ["sm1"])
+        ts(T.othird[:, 0:10], T.ms[:, 15:160:16], 16.0, T.pif[:], A.mult, A.add, ["ms", "pif"], ["oth"])
+        tt(T.rin[:], T.rs[:, 15:512:16], T.x2[:], A.add, ["rs", "x2"], ["rin"])
+        ts(T.sm[:, 2:3], T.ms[:, 15:16], o_(2), T.sh[:, 0:1], A.is_equal, A.mult, ["ms", "ob", "sm0"], ["sm2"])
+        for b in range(4):
+            tt(T.zl[:, b:256:4], plane(b).indirect(T.othird[:, 0:4]), T.aa[:, 160 * b:160 * b + 64], A.add,
+               ["hf%d" % b, "oth", "aa0%d" % b], ["zl%d" % b])
+        ts(T.sm[:, 3:4], o_(1), o_(0), 0.5, A.subtract, A.mult, ["ob"], ["sm3"])
+        quant(zq[:], zp[:], T.zl[:], four("zl") + ["zlp"], ["zq%d" % h])
+        for part in range(2):
+            rid, pid = topo.addr(to[part], core)
+            es = topo.engines(core, to[part])
+            es = es[:len(es) // 2] if part == 0 else es[len(es) // 2:]
+            if part == 0:
+                src = zq[:, 0:64].bitcast(dt.uint8)
+                dst = (qw[:, 0:64] if direct else T["rc%d" % h][:]).bitcast(dt.uint8)
+            else:
+                src = zp[:, 0:64]
+                dst = pw[:, 0:64] if direct else T["rp%d" % h][:]
+            op("g", lambda q, dst=dst, src=src, pid=pid, rid=rid, m=_mask(es), s=T.sem["arr%d" % h]: q.remote_dma(dst, src, s, T.sem.sent, pid, rid, m),
+               ["zq%d" % h], (), "remote")
+        op(None, None, (), ["arr%d" % h], "ext", "arr%d" % h, n_arr)
+        if h == 0:
+            iota(T.d0[:, 0:1024:2], [[0, 256], [-1, 2]], 0, 0, ["d02"], True)
+        act(T.kb[:, 0:1], T.sm[:, 2:3], ["sm1", "sm2"], ["kb0"], AF.Identity, bias=T.sm[:, 1:2])
+        steps = [(0, None)] + [(max(s - 2, 0), ((s + 1) // 2 + s) % 2) for s in range(1, 12)]
+        for s0 in range(0, 12, 2):
+            for s in (s0, s0 + 1):
+                fr, row = steps[s]
+                src = T.inid[:] if row is None else T.rin[:, 16 * row:16 * row + 16]
+                act(T.tw[:, 16 * s:16 * s + 16], src, ["rin", "inid", "kb%d" % fr], ["tw%d" % s], AF.Abs, bias=T.kb[:, fr:fr + 1])
+            for s in (s0, s0 + 1):
+                kw = {"accum_out": T.kb[:, s:s + 1]} if 0 < s < 10 else {}
+                act(T.zz[:, vv + s:vv + 256:16], T.tw[:, 16 * s:16 * s + 16], ["tw%d" % s, "zz"], ["vv%d" % s] + (["kb%d" % s] if kw else []),
+                    AF.Relu, bias=512.0, scale=-32.0, **kw)
+        act(T.d0[:, 1:1024:4], T.sg[:].indirect(T.linv[:, 0:16]), ["sg", "linv"], ["d01"], scale=-1.0 / 32.0)
+        act(T.d1[:, 1:1024:4], T.nn[:, 0:256], ["nn0", "sm3"], ["d11"], AF.Identity, scale=T.sm[:, 3:4])
+        for b in range(2, 4):
+            act(T.wn[:, WN * b + 160:WN * b + WN], plane(b), ["hf%d" % b], ["wg%d" % b], scale=64.0)
+        act(T.z32[:, 0:256], T.zl[:, 0:256], four("zl"), ["z320"], scale=32.0)
+        for b in range(4):
+            tt(T.ze[:, b:384:4], plane(b).indirect(T.othird[:, 4:10]), T.aa[:, 160 * b + 64:160 * b + 160], A.add,
+               ["hf%d" % b, "oth", "aa1%d" % b], ["ze%d" % b])
+        ts(T.rr[:, 16:32], T.rr[:, 0:16], -9.0, 30.0, A.add, A.mult, ["rr0"], ["rr1"])
+        quant(qw[:, 64:192], pw[:, 64:192], T.ze[:], four("ze") + ["zep"], ["qe%d" % h])
+        for b in range(4):
+            mm(2 + b, 128, T.wq[:, 128 * b:128 * b + 128], T.wp[:, 128 * b:128 * b + 128], qw[:, 64:192], pw[:, 64:192], ["wq", "wp", "qe%d" % h])
+        ts(T.z32[:, 256:640], T.ze[:, 0:384], 32.0, None, A.mult, None, four("ze"), ["z321"])
+        tt(T.rr[:, 32:48], T.rr[:, 0:16], T.rr[:, 16:32], A.max, ["rr0", "rr1"], ["rr2"])
+        tt(T.zz[:, rho:rho + 256:16], T.rin[:, 16:32], T.rin[:, 0:16], A.subtract, ["rin"], ["rho"])
+        tt(T.rr[:, 48:64], T.rr[:, 32:48], T.rkc[:, 16:32], A.min, ["rr2", "rkc1"], ["rr"])
+        for b in range(4):
+            tt(T.wn[:, WN * b + 64:WN * b + 160], bank(2 + b, 96), T.z32[:, 256 + b:640:4], A.add, ["z321"], ["we%d" % b, "b%d" % (2 + b)])
+        if h < R - 1:
+            ts(T.onew[:], T.rr[:, 48:64], 16.0, T.pif[:], A.mult, A.add, ["rr", "pif"], ["onew"])
+        else:
+            for k in range(2):
+                ts(T.of2[:, 16 * k:16 * k + 16], T.rr[:, 48:64], 16.0, T.pif[:], A.mult, A.add, ["rr", "pif"], ["of2%d" % k])
+            cp(T.lhalf[:], T.ipm[:, 2:4], ["ipm1"], ["lhalf"])
+        if h == 0:
+            ts(T.d1[:, 3:1024:4], tb[:], 0.5, None, A.mult, None, [ktb], ["d13"])
+        scan(T.vs[:], T.keep[:, 0:256], T.zz[:, vv:vv + 256], ["keep", "zz"] + ["vv%d" % s for s in range(12)], ["vs"])
+        scan(T.d1[:, 0:1024:4], T.keep[:, 0:256], T.zz[:, rho:rho + 256], ["keep", "rho"], ["d10"])
+        ts(T.zz[:, cs:cs + 256:16], T.vs[:, 15:256:16], 0.0, None, A.is_gt, None, ["vs"], ["cs"])
+        ts(T.d1[:, 2:1024:4], T.nn[:, 256:512], T.sm[:, 3:4], None, A.mult, None, ["nn1", "sm3"], ["d12"])
+        scan(T.d0[:, 3:1024:4], T.keep[:, 0:256], T.zz[:, cs:cs + 256], ["keep", "cs"], ["d03"])
+        if h == R - 1:
+            op("v", lambda q: q.transpose(T.oft[:], T.of2[:]), ["of20", "of21"], ["oft"])
+        elif h == 0:
+            ts(T.ltr[:], T.ib[:, 0:16], 4.0, 3.0, A.mult, A.add, ["ib0"], ["ltr"])
+        else:
+            ts(T.ipm[:, 2:4], T.ipart[:], 31, None, A.bitwise_and, None, ["ipart"], ["ipm1"])
+        scan(T.u4[:], T.d0[:], T.d1[:], ["d01", "d02", "d03", "d10", "d11", "d12", "d13"], ["u4"])
+        if h == 1:
+            quant(T.vq[:], T.vp[:], T.vin[:], ["vin"], ["vq"])
+        if h == R - 1:
+            cp(T.onew[:], T.oft[:].indirect(T.lhalf[:, 0:1]), ["oft", "lhalf"], ["onew"])
+        cp(T.uu[:], T.u4[:, 3:1024:4], ["u4"], ["uu"])
+        tt(tn[:], T.u4[:].indirect(T.ltr[:]), T.uu[:], A.add, ["u4", "uu", "ltr"], ["tb%d" % (h + 1)])
+        if h == R - 1:
+            dma("g", T.ot[:], tn[:], ["tb%d" % R], ["ot"])
+        lb = [6, 7, 0, 1]
+        for b in range(4):
+            mm(lb[b], 128, T.wq[:, 128 * b:128 * b + 128], T.wp[:, 128 * b:128 * b + 128], qw[:, 0:128], pw[:, 0:128], ["wq", "wp", "qe%d" % h, "arr%d" % h])
+        for b in range(4):
+            tt(T.wn[:, WN * b:WN * b + 64], bank(lb[b], 64), T.z32[:, b:256:4], A.add, ["z320"], ["wl%d" % b, "b%d" % lb[b]])
+        for b in range(4):
+            win = T.wn[:, WN * b:WN * b + WN].indirect(T.onew[:])
+            rd = ["wl%d" % b, "we%d" % b, "wg%d" % b, "onew"]
+            if b < 2:
+                act(T.xn[:, b:1024:4], win, rd, ["xn%d" % b], scale=0.03125)
+            else:
+                ts(T.xn[:, b:1024:4], win, 0.03125, None, A.mult, None, rd, ["xn%d" % b])
+        nc, ns = T["xc%d" % (h + 1)], T["xs%d" % (h + 1)]
+        for k in range(2):
+            quant(nc[:, 128 * k:128 * k + 128], ns[:, 128 * k:128 * k + 128], T.xn[:, 512 * k:512 * k + 512],
+                  four("xn"), ["xc%d%d" % (h + 1, k), "xs%d%d" % (h + 1, k)])
+    xc, xs = T["xc%d" % R], T["xs%d" % R]
+    kx = [["xc%d%d" % (R, k), "xs%d%d" % (R, k)] for k in range(2)]
+    for k in range(2):
+        mm(2 + k, 128, T.vq[:], T.vp[:], xc[:, 128 * k:128 * k + 128], xs[:, 128 * k:128 * k + 128], ["vq"] + kx[k])
+    dma("s", T.oc[:], xc[:].bitcast(dt.uint8), kx[0] + kx[1], ["oc"])
+    act(T.yo[:, 0:128], bank(2, 128), (), ["yo0", "b2"])
+    cp(T.yo[:, 128:256], bank(3, 128), (), ["yo1", "b3"])
+    for k in range(4):
+        dma("g" if k < 2 else "s", T.osc[4 * k:4 * k + 4, :], xs[32 * k:32 * k + 4, :], kx[0] + kx[1], ["os%d" % k])
+    dma("a", T.y[:], T.yo[:], ["yo0", "yo1"], ["y"])
+    op("g", None, ["oc", "y", "ot"] + four("os"), ())
+    _emit(g, T, ops)
+    g.wait_ge(T.sem.sent, R * sum(len(topo.engines(core, c)) // 2 for c in to))

@@ -222,26 +222,28 @@ def rank_program(g, core, T, topo):
     fill(T.rk[:, 255:256], 16.0, ["rkp"])
     fill(T.keep[:, 0:272:16], 0.0, ["keep"])
     fill(T.flip[:, 0:240:16], 0.0, ["flip"])
+    cp(T.lu[:], T.icol[:], ["icol"], ["lu"])
     cp(T.ebig[:, 3:515:4], T.ident[:], ["ident"], ["ebig"])
     fill(T.flip[:, 15:240:15], -1.0, ["flip"])
-    cp(T.lu[:], T.icol[:], ["icol"], ["lu"])
     ts(T.ib[:, 0:16], T.ia[:, 0:16], 255, None, A.bitwise_and, None, ["ia0"], ["ib0"])
     for b in range(4):
         quant(T.eq[:, 128 * b:128 * b + 128], T.ep[:, 128 * b:128 * b + 128], T.ebig[:, 3 - b:515 - b], ["ebig"], ["e%d" % b])
     cp(T.lx[:], T.ib[:, 0:16], ["ib0"], ["lx"])
     ts(T.ipm[:, 0:2], T.ipart[:], 15, None, A.bitwise_and, None, ["ipart"], ["ipm0"])
     ts(T.ib[:, 16:48], T.ia[:, 16:48], 255, None, A.bitwise_and, None, ["ia1", "ia2"], ["ib1"])
-    cp(T.pif[:], T.ipm[:, 0:1], ["ipm0"], ["pif"])
     quant(T.uq0[:], T.up0[:], T.uin[:], ["uin"], ["uq0"])
+    cp(T.pif[:], T.ipm[:, 0:1], ["ipm0"], ["pif"])
     tt(T.ic[:, 0:16], T.ib[:, 16:32], T.icol[:], A.min, ["ib1", "icol"], ["ic0"])
     cp(T.uq[:].bitcast(u32), T.uq0[:].bitcast(u32).indirect(T.lu[:, 0:8]), ["uq0", "lu"], ["uq"])
     act(T.up[:], T.up0[:].indirect(T.lu[:, 0:8]), ["uq0", "lu"], ["up"])
     quant(T.xq0[:], T.xp0[:], T.xin[:], ["xin"], ["xq0"])
     tt(T.ic[:, 16:32], T.ib[:, 16:32], T.icol[:], A.max, ["ib1", "icol"], ["ic1"])
+    ts(T.msk[:], T.yi[:], T.pif[:], None, A.is_equal, None, ["yi", "pif"], ["msk"])
     for k in range(2):
         cp(T.xc0[:, 128 * k:128 * k + 128].bitcast(u32), T.xq0[:].bitcast(u32).indirect(T.lx[:, 8 * k:8 * k + 8]), ["xq0", "lx"], ["xc0%d" % k])
         act(T.xs0[:, 128 * k:128 * k + 128], T.xp0[:].indirect(T.lx[:, 8 * k:8 * k + 8]), ["xq0", "lx"], ["xs0%d" % k])
-    ts(T.msk[:], T.yi[:], T.pif[:], None, A.is_equal, None, ["yi", "pif"], ["msk"])
+    ts(T.lcmp[:], T.ic[:], 15.0, None, A.add, None, ["ic0", "ic1"], ["lcmp"])
+    cp(T.linv[:], T.ib[:, 32:48], ["ib1"], ["linv"])
 
     def o_(j):
         return T.ob[:, 16 * j + 15:16 * j + 16]
@@ -249,28 +251,41 @@ def rank_program(g, core, T, topo):
     def plane(b):
         return T.hf[:, 256 * b:256 * b + 256]
 
+    def switch_u():
+        scan(T.u4[:], T.d0[:], T.d1[:], ["d01", "d02", "d03", "d10", "d11", "d12", "d13"], ["u4"])
+
+    def switch_copy():
+        cp(T.uu[:], T.u4[:, 3:1024:4], ["u4"], ["uu"])
+
+    def switch_new(k):
+        tt(T["tb%d" % k][:], T.u4[:].indirect(T.ltr[:]), T.uu[:], A.add, ["u4", "uu", "ltr"], ["tb%d" % k])
+
     for h in range(R):
         xc, xs = T["xc%d" % h], T["xs%d" % h]
         kx = [["xc%d%d" % (h, k), "xs%d%d" % (h, k)] for k in range(2)]
-        tb, tn = T["tb%d" % h], T["tb%d" % (h + 1)]
+        tb = T["tb%d" % h]
         ktb = "tb%d" % h
         zq, zp, qw, pw = T["zq%d" % h], T["zp%d" % h], T["qw%d" % h], T["pw%d" % h]
         for k in range(2):
             mm(k, 128, T.uq[:], T.up[:], xc[:, 128 * k:128 * k + 128], xs[:, 128 * k:128 * k + 128], ["uq", "up"] + kx[k])
         for b in range(4):
             mm(2 + b, 256, T.eq[:, 128 * b:128 * b + 128], T.ep[:, 128 * b:128 * b + 128], xc[:], xs[:], ["e%d" % b] + kx[0] + kx[1])
+        if h > 0:
+            switch_u()
         tt(T.mb[:, 0:128], bank(0, 128), T.msk[:, 0:128], A.mult, ["msk"], ["mb0", "b0"])
         tt(T.mb[:, 128:240], bank(1, 112), T.msk[:, 128:240], A.mult, ["msk"], ["mb1", "b1"])
-        if h == 0:
-            ts(T.lcmp[:], T.ic[:], 15.0, None, A.add, None, ["ic0", "ic1"], ["lcmp"])
+        if h > 0:
+            switch_copy()
         else:
-            act(T.d1[:, 3:1024:4], tb[:], [ktb], ["d13"], scale=0.5)
+            ts(T.ltr[:], T.ib[:, 0:16], 4.0, 3.0, A.mult, A.add, ["ib0"], ["ltr"])
         act(plane(0), bank(2, 256), (), ["hf0", "b2"], scale=0.5)
         scan(T.sc[:, 0:240], T.keep[:, 0:240], T.mb[:], ["keep", "mb0", "mb1"], ["sc"])
         if h == 0:
-            cp(T.linv[:], T.ib[:, 32:48], ["ib1"], ["linv"])
+            ts(T.ipm[:, 2:4], T.ipart[:], 31, None, A.bitwise_and, None, ["ipart"], ["ipm1"])
         cp(T.g1[:, 0:128], T.sc[:].indirect(T.lcmp[:, 16:24]), ["sc", "scp", "lcmp"], ["g1a"])
         act(T.g1[:, 128:240], T.sc[:].indirect(T.lcmp[:, 24:31]), ["sc", "scp", "lcmp"], ["g1b"])
+        if h == 0:
+            cp(T.lhalf[:], T.ipm[:, 2:4], ["ipm1"], ["lhalf"])
         tt(T.cm[:], T.sc[:].indirect(T.lcmp[:, 0:15]), T.g1[:], A.is_ge, ["sc", "scp", "lcmp", "g1a", "g1b"], ["cm"])
         for b in range(1, 4):
             act(plane(b), bank(2 + b, 256), (), ["hf%d" % b, "b%d" % (2 + b)], scale=0.5)
@@ -278,13 +293,16 @@ def rank_program(g, core, T, topo):
             act(T.wn[:, WN * b + 160:WN * b + WN], plane(b), ["hf%d" % b], ["wg%d" % b], scale=64.0)
         if h == 0:
             cp(T.tb0[:], T.tin[:], ["tin"], ["tb0"])
+        else:
+            switch_new(h)
         scan(T.rk[:, 0:240], T.flip[:], T.cm[:], ["flip", "cm"], ["rk"])
         tt(T.nq[:], T.rk[:].indirect(T.linv[:, 0:11]), T.targ[:], A.not_equal, ["rk", "rkp", "linv", "targ"], ["nq"])
         tt(T.rr[:, 0:16], T.rk[:, 15:256:16], T.rkc[:, 0:16], A.add, ["rk", "rkp", "rkc0"], ["rr0"])
         scan(T.ob[:], T.nq[:], T.keep[:, 1:177], ["nq", "keep"], ["ob"])
         tt(T.sg[:, 15:256:16], T.nq[:, 16:32], T.nq[:, 0:16], A.subtract, ["nq"], ["sg"])
-        ts(T.osec[:, 0:10], T.ob[:, 31:176:16], 16.0, T.pif[:], A.mult, A.add, ["ob", "pif"], ["osec"])
+        ts(T.rr[:, 16:32], T.rr[:, 0:16], -9.0, 30.0, A.add, A.mult, ["rr0"], ["rr1"])
         ts(T.o16[:, 0:10], T.ob[:, 15:160:16], 16.0, None, A.mult, None, ["ob"], ["o16"])
+        ts(T.osec[:, 0:10], T.ob[:, 31:176:16], 16.0, T.pif[:], A.mult, A.add, ["ob", "pif"], ["osec"])
         for b in range(4):
             act(T.aa[:, 160 * b:160 * b + 64], plane(b).indirect(T.osec[:, 0:4]), ["hf%d" % b, "osec"], ["aa0%d" % b])
         for b in range(4):
@@ -292,19 +310,22 @@ def rank_program(g, core, T, topo):
         ts(T.nn[:, 0:256], tb[:], o_(0), None, A.not_equal, None, [ktb, "ob"], ["nn0"])
         tt(T.o16[:, 16:26], T.o16[:, 0:10], T.ob[:, 31:176:16], A.add, ["ob", "o16"], ["o17"])
         ts(T.nn[:, 256:512], tb[:], o_(1), None, A.not_equal, None, [ktb, "ob"], ["nn1"])
-        cp(T.oidx[:, 0:10], T.o16[:, 16:26], ["o17"], ["oidx"])
         ts(T.sh[:, 0:1], o_(3), o_(2), -32.0, A.subtract, A.mult, ["ob"], ["sm0"])
-        tt(T.lk[:], tb[:].indirect(T.oidx[:, 0:10]), T.msk[:, 0:160], A.mult, [ktb, "msk", "oidx"], ["lk"])
+        cp(T.oidx[:, 0:10], T.o16[:, 16:26], ["o17"], ["oidx"])
         scan(T.rs[:], T.nn[:], T.m32[:], ["nn0", "nn1", "m32"], ["rs"])
-        scan(T.ms[:], T.keep[:, 0:160], T.lk[:], ["keep", "lk"], ["ms"])
-        ts(T.sm[:, 1:2], o_(2), -32.0, 512.0, A.mult, A.add, ["ob"], ["sm1"])
-        ts(T.othird[:, 0:10], T.ms[:, 15:160:16], 16.0, T.pif[:], A.mult, A.add, ["ms", "pif"], ["oth"])
+        tt(T.lk[:], tb[:].indirect(T.oidx[:, 0:10]), T.msk[:, 0:160], A.mult, [ktb, "msk", "oidx"], ["lk"])
         tt(T.rin[:], T.rs[:, 15:512:16], T.x2[:], A.add, ["rs", "x2"], ["rin"])
+        ts(T.sm[:, 1:2], o_(2), -32.0, 512.0, A.mult, A.add, ["ob"], ["sm1"])
+        scan(T.ms[:], T.keep[:, 0:160], T.lk[:], ["keep", "lk"], ["ms"])
+        ts(T.sm[:, 3:4], o_(1), o_(0), 0.5, A.subtract, A.mult, ["ob"], ["sm3"])
+        tt(T.rr[:, 32:48], T.rr[:, 0:16], T.rr[:, 16:32], A.max, ["rr0", "rr1"], ["rr2"])
+        ts(T.othird[:, 0:10], T.ms[:, 15:160:16], 16.0, T.pif[:], A.mult, A.add, ["ms", "pif"], ["oth"])
         ts(T.sm[:, 2:3], T.ms[:, 15:16], o_(2), T.sh[:, 0:1], A.is_equal, A.mult, ["ms", "ob", "sm0"], ["sm2"])
+        tt(T.zz[:, rho:rho + 256:16], T.rin[:, 16:32], T.rin[:, 0:16], A.subtract, ["rin"], ["rho"])
         for b in range(4):
             tt(T.zl[:, b:256:4], plane(b).indirect(T.othird[:, 0:4]), T.aa[:, 160 * b:160 * b + 64], A.add,
                ["hf%d" % b, "oth", "aa0%d" % b], ["zl%d" % b])
-        ts(T.sm[:, 3:4], o_(1), o_(0), 0.5, A.subtract, A.mult, ["ob"], ["sm3"])
+        tt(T.rr[:, 48:64], T.rr[:, 32:48], T.rkc[:, 16:32], A.min, ["rr2", "rkc1"], ["rr"])
         quant(zq[:], zp[:], T.zl[:], four("zl") + ["zlp"], ["zq%d" % h])
         for part in range(2):
             rid, pid = topo.addr(to[part], core)
@@ -332,57 +353,41 @@ def rank_program(g, core, T, topo):
                 kw = {"accum_out": T.kb[:, s:s + 1]} if 0 < s < 10 else {}
                 act(T.zz[:, vv + s:vv + 256:16], T.tw[:, 16 * s:16 * s + 16], ["tw%d" % s, "zz"], ["vv%d" % s] + (["kb%d" % s] if kw else []),
                     AF.Relu, bias=512.0, scale=-32.0, **kw)
-        act(T.d0[:, 1:1024:4], T.sg[:].indirect(T.linv[:, 0:16]), ["sg", "linv"], ["d01"], scale=-1.0 / 32.0)
-        act(T.d1[:, 1:1024:4], T.nn[:, 0:256], ["nn0", "sm3"], ["d11"], AF.Identity, scale=T.sm[:, 3:4])
-        for b in range(2, 4):
-            act(T.wn[:, WN * b + 160:WN * b + WN], plane(b), ["hf%d" % b], ["wg%d" % b], scale=64.0)
-        act(T.z32[:, 0:256], T.zl[:, 0:256], four("zl"), ["z320"], scale=32.0)
+            if s0 in (0, 2):
+                b = 2 + s0 // 2
+                act(T.wn[:, WN * b + 160:WN * b + WN], plane(b), ["hf%d" % b], ["wg%d" % b], scale=64.0)
+            elif s0 == 4:
+                act(T.z32[:, 0:256], T.zl[:, 0:256], four("zl"), ["z320"], scale=32.0)
         for b in range(4):
             tt(T.ze[:, b:384:4], plane(b).indirect(T.othird[:, 4:10]), T.aa[:, 160 * b + 64:160 * b + 160], A.add,
                ["hf%d" % b, "oth", "aa1%d" % b], ["ze%d" % b])
-        ts(T.rr[:, 16:32], T.rr[:, 0:16], -9.0, 30.0, A.add, A.mult, ["rr0"], ["rr1"])
+        scan(T.d1[:, 0:1024:4], T.keep[:, 0:256], T.zz[:, rho:rho + 256], ["keep", "rho"], ["d10"])
         quant(qw[:, 64:192], pw[:, 64:192], T.ze[:], four("ze") + ["zep"], ["qe%d" % h])
         for b in range(4):
             mm(2 + b, 128, T.wq[:, 128 * b:128 * b + 128], T.wp[:, 128 * b:128 * b + 128], qw[:, 64:192], pw[:, 64:192], ["wq", "wp", "qe%d" % h])
         ts(T.z32[:, 256:640], T.ze[:, 0:384], 32.0, None, A.mult, None, four("ze"), ["z321"])
-        tt(T.rr[:, 32:48], T.rr[:, 0:16], T.rr[:, 16:32], A.max, ["rr0", "rr1"], ["rr2"])
-        tt(T.zz[:, rho:rho + 256:16], T.rin[:, 16:32], T.rin[:, 0:16], A.subtract, ["rin"], ["rho"])
-        tt(T.rr[:, 48:64], T.rr[:, 32:48], T.rkc[:, 16:32], A.min, ["rr2", "rkc1"], ["rr"])
-        for b in range(4):
-            tt(T.wn[:, WN * b + 64:WN * b + 160], bank(2 + b, 96), T.z32[:, 256 + b:640:4], A.add, ["z321"], ["we%d" % b, "b%d" % (2 + b)])
+        ts(T.d1[:, 1:1024:4], T.nn[:, 0:256], T.sm[:, 3:4], None, A.mult, None, ["nn0", "sm3"], ["d11"])
         if h < R - 1:
             ts(T.onew[:], T.rr[:, 48:64], 16.0, T.pif[:], A.mult, A.add, ["rr", "pif"], ["onew"])
         else:
             for k in range(2):
                 ts(T.of2[:, 16 * k:16 * k + 16], T.rr[:, 48:64], 16.0, T.pif[:], A.mult, A.add, ["rr", "pif"], ["of2%d" % k])
-            cp(T.lhalf[:], T.ipm[:, 2:4], ["ipm1"], ["lhalf"])
-        if h == 0:
-            ts(T.d1[:, 3:1024:4], tb[:], 0.5, None, A.mult, None, [ktb], ["d13"])
-        scan(T.vs[:], T.keep[:, 0:256], T.zz[:, vv:vv + 256], ["keep", "zz"] + ["vv%d" % s for s in range(12)], ["vs"])
-        scan(T.d1[:, 0:1024:4], T.keep[:, 0:256], T.zz[:, rho:rho + 256], ["keep", "rho"], ["d10"])
-        ts(T.zz[:, cs:cs + 256:16], T.vs[:, 15:256:16], 0.0, None, A.is_gt, None, ["vs"], ["cs"])
-        ts(T.d1[:, 2:1024:4], T.nn[:, 256:512], T.sm[:, 3:4], None, A.mult, None, ["nn1", "sm3"], ["d12"])
-        scan(T.d0[:, 3:1024:4], T.keep[:, 0:256], T.zz[:, cs:cs + 256], ["keep", "cs"], ["d03"])
+        for b in range(4):
+            tt(T.wn[:, WN * b + 64:WN * b + 160], bank(2 + b, 96), T.z32[:, 256 + b:640:4], A.add, ["z321"], ["we%d" % b, "b%d" % (2 + b)])
         if h == R - 1:
             op("v", lambda q: q.transpose(T.oft[:], T.of2[:]), ["of20", "of21"], ["oft"])
-        elif h == 0:
-            ts(T.ltr[:], T.ib[:, 0:16], 4.0, 3.0, A.mult, A.add, ["ib0"], ["ltr"])
-        else:
-            ts(T.ipm[:, 2:4], T.ipart[:], 31, None, A.bitwise_and, None, ["ipart"], ["ipm1"])
-        scan(T.u4[:], T.d0[:], T.d1[:], ["d01", "d02", "d03", "d10", "d11", "d12", "d13"], ["u4"])
+        ts(T.d1[:, 2:1024:4], T.nn[:, 256:512], T.sm[:, 3:4], None, A.mult, None, ["nn1", "sm3"], ["d12"])
         if h == 1:
             quant(T.vq[:], T.vp[:], T.vin[:], ["vin"], ["vq"])
         if h == R - 1:
             cp(T.onew[:], T.oft[:].indirect(T.lhalf[:, 0:1]), ["oft", "lhalf"], ["onew"])
-        cp(T.uu[:], T.u4[:, 3:1024:4], ["u4"], ["uu"])
-        tt(tn[:], T.u4[:].indirect(T.ltr[:]), T.uu[:], A.add, ["u4", "uu", "ltr"], ["tb%d" % (h + 1)])
-        if h == R - 1:
-            dma("g", T.ot[:], tn[:], ["tb%d" % R], ["ot"])
+        ts(T.d1[:, 3:1024:4], tb[:], 0.5, None, A.mult, None, [ktb], ["d13"])
         lb = [6, 7, 0, 1]
         for b in range(4):
             mm(lb[b], 128, T.wq[:, 128 * b:128 * b + 128], T.wp[:, 128 * b:128 * b + 128], qw[:, 0:128], pw[:, 0:128], ["wq", "wp", "qe%d" % h, "arr%d" % h])
         for b in range(4):
             tt(T.wn[:, WN * b:WN * b + 64], bank(lb[b], 64), T.z32[:, b:256:4], A.add, ["z320"], ["wl%d" % b, "b%d" % lb[b]])
+        scan(T.vs[:], T.keep[:, 0:256], T.zz[:, vv:vv + 256], ["keep", "zz"] + ["vv%d" % s for s in range(12)], ["vs"])
         for b in range(4):
             win = T.wn[:, WN * b:WN * b + WN].indirect(T.onew[:])
             rd = ["wl%d" % b, "we%d" % b, "wg%d" % b, "onew"]
@@ -390,6 +395,10 @@ def rank_program(g, core, T, topo):
                 act(T.xn[:, b:1024:4], win, rd, ["xn%d" % b], scale=0.03125)
             else:
                 ts(T.xn[:, b:1024:4], win, 0.03125, None, A.mult, None, rd, ["xn%d" % b])
+            if b == 2:
+                ts(T.zz[:, cs:cs + 256:16], T.vs[:, 15:256:16], 0.0, None, A.is_gt, None, ["vs"], ["cs"])
+        act(T.d0[:, 1:1024:4], T.sg[:].indirect(T.linv[:, 0:16]), ["sg", "linv"], ["d01"], scale=-1.0 / 32.0)
+        scan(T.d0[:, 3:1024:4], T.keep[:, 0:256], T.zz[:, cs:cs + 256], ["keep", "cs"], ["d03"])
         nc, ns = T["xc%d" % (h + 1)], T["xs%d" % (h + 1)]
         for k in range(2):
             quant(nc[:, 128 * k:128 * k + 128], ns[:, 128 * k:128 * k + 128], T.xn[:, 512 * k:512 * k + 512],
@@ -398,12 +407,16 @@ def rank_program(g, core, T, topo):
     kx = [["xc%d%d" % (R, k), "xs%d%d" % (R, k)] for k in range(2)]
     for k in range(2):
         mm(2 + k, 128, T.vq[:], T.vp[:], xc[:, 128 * k:128 * k + 128], xs[:, 128 * k:128 * k + 128], ["vq"] + kx[k])
+    switch_u()
     dma("s", T.oc[:], xc[:].bitcast(dt.uint8), kx[0] + kx[1], ["oc"])
-    act(T.yo[:, 0:128], bank(2, 128), (), ["yo0", "b2"])
-    cp(T.yo[:, 128:256], bank(3, 128), (), ["yo1", "b3"])
+    for k in range(2):
+        act(T.yo[:, 128 * k:128 * k + 128], bank(2 + k, 128), (), ["yo%d" % k, "b%d" % (2 + k)])
+    switch_copy()
+    switch_new(R)
     for k in range(4):
         dma("g" if k < 2 else "s", T.osc[4 * k:4 * k + 4, :], xs[32 * k:32 * k + 4, :], kx[0] + kx[1], ["os%d" % k])
     dma("a", T.y[:], T.yo[:], ["yo0", "yo1"], ["y"])
+    dma("s", T.ot[:], T.tb3[:], ["tb%d" % R], ["ot"])
     op("g", None, ["oc", "y", "ot"] + four("os"), ())
     _emit(g, T, ops)
     g.wait_ge(T.sem.sent, R * sum(len(topo.engines(core, c)) // 2 for c in to))

@@ -3,12 +3,13 @@ from concourse.mybir import dt, AluOpType, ActivationFunctionType
 R = 3
 F8, U8, BF, F32, I32, U16 = "float8_e4m3fn_x4", "uint8", "bfloat16", "float32", "int32", "uint16"
 WN = 416
+LIFT = 64.0
 
 _SB = {
-    BF: dict(xin=1024, uin=512, vin=512, ones=128, ident=128, ebig=528, yi=256, msk=256, keep=272, flip=240, targ=176, m32=512,
+    BF: dict(xin=1024, uin=512, vin=512, ones=128, ident=128, ebig=528, yi=256, msk=256, keep=272, flip=240, targ=176, c16=256,
              cm=240, rk=256, nq=176, ob=176, lk=160, ms=160, hf=1024, aa=640, zl=512, ze=512, z32=640, wn=4 * WN, xn=1024,
-             nn=512, rs=512, sg=256, sh=2, zz=768, vs=256, d0=1024, d1=1024, u4=1024, uu=256, tb0=256, tb1=256, tb2=256),
-    F32: dict(pif=1, x2=32, inid=16, rkc=32, mb=240, sc=256, g1=240, o16=32, rr=64, of2=32, oft=32, rin=32, sm=8, kb=16, tw=192,
+             rs=512, sg=256, sh=2, zz=768, vs=256, d0=1024, ub0=1024, ub1=1024, ut=256, tb0=256, tb1=256, tb2=256),
+    F32: dict(pif=1, x2=32, x2s=32, inid=16, rkc=32, mb=240, sc=256, g1=240, sx=16, rr=64, of2=32, oft=32, rin=32, sm=8, kb=16, tw=192,
               tb3=256, yo=256),
     I32: dict(tin=256, ia=48, ib=48, ic=32, icol=16, ipart=2, ipm=4),
     U16: dict(lx=16, lu=16, lcmp=32, linv=16, ltr=16, lhalf=2, osec=16, oidx=16, othird=16, onew=16),
@@ -29,6 +30,15 @@ SEMAPHORES = ["cv", "ca", "ct", "cg", "sent"] + ["arr%d" % h for h in range(R)] 
 A = AluOpType
 AF = ActivationFunctionType
 
+ORDER = {
+    "v": """vs- cs- mb0 mb1 d03- sc0 sc1 u- ltr tb0 cma cmb rka rkb ipm1 add- nqE nqL obE obL sxE osecE uinit oidxE n0 n1 lkE osecL rs1 msE rs0 sxL
+            othE sm2 rin oidxL zl0 zl1 zl2 zl3 lkL qz lhalf msL rr0 sig othL sg rr1 ze0 ze1 ze2 ze3 rho rr2 qe rr3 d10 z32e of20 of21 oft
+            we0 we1 onewT onew vq we2 we3 wl0 wl1 wl2 wl3 xn2 xn3 q0 q1""",
+    "a": """g1a g1b ut- hf0 hf1 hf2 dab t23 hf3 aE0 aE1 sh aE2 aE3 aL0 aL1 aL2 kb0 aL3 A1 wg0 B1 A2 A0 wg1 B2 A3 A4 B3 s64 A5 B0 B5 B4 A7 A6 B7
+            z32l A9 B6 wg2 B9 A8 wg3 A11 B8 xn0 xn1 A10 B11 B10 d01""",
+}
+TAIL = {"v": "vs- cs- d03- u- yo0 yo1 add-", "a": "os2 os3 ut- y"}
+
 
 def _mask(es):
     m = 0
@@ -42,69 +52,86 @@ def _relays(src, dst, group, topo):
     return sorted(cs, key=lambda c: (topo.die(c) != topo.die(src), c))[:2]
 
 
+def _queues(ops):
+    at = {(o["h"], o["name"]): i for i, o in enumerate(ops) if o["name"]}
+    qs = {}
+    for e in ("v", "a", "t", "g", "s", None):
+        if e not in ORDER:
+            qs[e] = [i for i, o in enumerate(ops) if o["e"] == e]
+            continue
+        qs[e] = [i for i, o in enumerate(ops) if o["e"] == e and not o["name"]]
+        for h in range(R + 1):
+            for w in (ORDER[e] if h < R else TAIL[e]).split():
+                k = (h - 1, w[:-1]) if w.endswith("-") else (h, w)
+                if k in at and at[k] not in qs[e]:
+                    qs[e].append(at[k])
+        assert sorted(qs[e]) == [i for i, o in enumerate(ops) if o["e"] == e]
+    return qs
+
+
 def _emit(g, T, ops):
     q = {"v": g.vector, "a": g.scalar, "t": g.tensor, "g": g, "s": g.sync}
     cs = {"v": "cv", "a": "ca", "t": "ct", "g": "cg"}
-    lastw, readers = {}, {}
-    known = {e: ({}, set()) for e in q}
-    snap, waits, sig = [], [], set()
+    lastw, readers, deps = {}, {}, []
     for i, o in enumerate(ops):
-        e = o["e"]
-        deps = set()
-        for k in o["r"]:
-            if k in lastw:
-                deps.add(lastw[k])
+        d = set(lastw[k] for k in o["r"] + o["w"] if k in lastw)
         for k in o["w"]:
-            if k in lastw:
-                deps.add(lastw[k])
-            deps.update(readers.get(k, []))
-        w = []
-        if e is not None:
-            kc, ks = known[e]
-            for d in sorted(deps, reverse=True):
-                p = ops[d]
-                if p["sem"] is None:
-                    if kc.get(p["e"], -1) >= d:
-                        continue
-                    kc[p["e"]] = d
-                elif d in ks:
-                    continue
-                else:
-                    ks.add(d)
-                w.append(d)
-                sig.add(d)
-                for k2, v2 in snap[d][0].items():
-                    if kc.get(k2, -1) < v2:
-                        kc[k2] = v2
-                ks.update(snap[d][1])
-            snap.append((dict(kc), set(ks)))
-        else:
-            snap.append(({}, set()))
-        waits.append(w)
+            d.update(readers.get(k, []))
+        deps.append(d)
         for k in o["r"]:
             readers.setdefault(k, []).append(i)
         for k in o["w"]:
             lastw[k] = i
             readers[k] = []
-    cnt, val = {e: 0 for e in cs}, {}
-    for i, o in enumerate(ops):
-        if o["sem"] is None and i in sig:
-            cnt[o["e"]] += 1
-            val[i] = (cs[o["e"]], cnt[o["e"]])
-        elif o["sem"] is not None:
-            val[i] = (o["sem"], o["n"])
-    for i, o in enumerate(ops):
-        if o["e"] is None:
-            continue
-        for d in waits[i]:
-            q[o["e"]].wait_ge(T.sem[val[d][0]], val[d][1])
-        if o["f"] is None:
-            continue
-        ins = o["f"](q[o["e"]])
-        if o["kind"] == "dma":
-            ins.then_inc(T.sem[o["sem"]], 16)
-        elif o["kind"] == "c" and i in sig:
-            ins.then_inc(T.sem[val[i][0]], 1)
+    qs = _queues(ops)
+    pos = {i: n for e in qs for n, i in enumerate(qs[e])}
+    known = {e: ({}, set()) for e in q}
+    snap = {i: ({}, set()) for i in qs[None]}
+    waits, sig, nxt = {}, set(), {e: 0 for e in q}
+    moved = True
+    while moved:
+        moved = False
+        for e in q:
+            while nxt[e] < len(qs[e]) and all(d in snap for d in deps[qs[e][nxt[e]]]):
+                i = qs[e][nxt[e]]
+                nxt[e] += 1
+                moved = True
+                kc, ks = known[e]
+                waits[i] = []
+                for d in sorted(deps[i], key=lambda d: -pos[d]):
+                    p = ops[d]
+                    if p["sem"] is None:
+                        if kc.get(p["e"], -1) >= pos[d]:
+                            continue
+                        kc[p["e"]] = pos[d]
+                    elif d in ks:
+                        continue
+                    else:
+                        ks.add(d)
+                    waits[i].append(d)
+                    sig.add(d)
+                    for k2, v2 in snap[d][0].items():
+                        if kc.get(k2, -1) < v2:
+                            kc[k2] = v2
+                    ks.update(snap[d][1])
+                snap[i] = (dict(kc), set(ks))
+    assert all(nxt[e] == len(qs[e]) for e in q)
+    val = {i: (o["sem"], o["n"]) for i, o in enumerate(ops) if o["sem"] is not None}
+    for e in cs:
+        for n, i in enumerate([i for i in qs[e] if ops[i]["sem"] is None and i in sig]):
+            val[i] = (cs[e], n + 1)
+    for e in q:
+        for i in qs[e]:
+            o = ops[i]
+            for d in waits[i]:
+                q[e].wait_ge(T.sem[val[d][0]], val[d][1])
+            if o["f"] is None:
+                continue
+            ins = o["f"](q[e])
+            if o["kind"] == "dma":
+                ins.then_inc(T.sem[o["sem"]], 16)
+            elif o["kind"] == "c" and i in sig:
+                ins.then_inc(T.sem[val[i][0]], 1)
 
 
 def _relay_program(g, core, T, topo, dst, part):
@@ -143,46 +170,47 @@ def rank_program(g, core, T, topo):
 
     ops = []
     ndma = [0]
+    now = [0]
 
-    def op(e, f, r=(), w=(), kind="c", sem=None, cnt=0):
-        ops.append({"e": e, "f": f, "r": list(r), "w": list(w), "kind": kind, "sem": sem, "n": cnt})
+    def op(nm, e, f, r=(), w=(), kind="c", sem=None, cnt=0):
+        ops.append({"name": nm, "h": now[0], "e": e, "f": f, "r": list(r), "w": list(w), "kind": kind, "sem": sem, "n": cnt})
 
-    def dma(e, out, in_, r=(), w=()):
-        op(e, lambda q: q.dma_start(out, in_), r, w, "dma", "dm%d" % ndma[0], 16)
+    def dma(nm, e, out, in_, r=(), w=()):
+        op(nm, e, lambda q: q.dma_start(out, in_), r, w, "dma", "dm%d" % ndma[0], 16)
         ndma[0] += 1
 
-    def ts(out, in0, s1, s2, o0, o1, r, w):
+    def ts(nm, out, in0, s1, s2, o0, o1, r, w):
         if o1 is None:
-            op("v", lambda q: q.tensor_scalar(out, in0, s1, None, o0), r, w)
+            op(nm, "v", lambda q: q.tensor_scalar(out, in0, s1, None, o0), r, w)
         else:
-            op("v", lambda q: q.tensor_scalar(out, in0, s1, s2, o0, o1), r, w)
+            op(nm, "v", lambda q: q.tensor_scalar(out, in0, s1, s2, o0, o1), r, w)
 
-    def tt(out, a, b, o, r, w):
-        op("v", lambda q: q.tensor_tensor(out, a, b, o), r, w)
+    def tt(nm, out, a, b, o, r, w):
+        op(nm, "v", lambda q: q.tensor_tensor(out, a, b, o), r, w)
 
-    def scan(out, a, b, r, w):
-        op("v", lambda q: q.tensor_tensor_scan(out, a, b, 0.0, A.mult, A.add), r, w)
+    def scan(nm, out, a, b, r, w, o0=A.mult, first=0.0):
+        op(nm, "v", lambda q: q.tensor_tensor_scan(out, a, b, first, o0, A.add), r, w)
 
-    def cp(out, a, r, w):
-        op("v", lambda q: q.tensor_copy(out, a), r, w)
+    def cp(nm, out, a, r, w):
+        op(nm, "v", lambda q: q.tensor_copy(out, a), r, w)
 
     def fill(ap, c, w):
-        op("v", lambda q: q.memset(ap, c), (), w)
+        op(None, "v", lambda q: q.memset(ap, c), (), w)
 
-    def act(out, a, r, w, func=AF.Copy, **kw):
-        op("a", lambda q: q.activation(out, a, func, **kw), r, w)
+    def act(nm, out, a, r, w, func=AF.Copy, **kw):
+        op(nm, "a", lambda q: q.activation(out, a, func, **kw), r, w)
 
-    def quant(c, s, a, r, w):
-        op("v", lambda q: q.quantize_mx(c, s, a), r, w)
+    def quant(nm, c, s, a, r, w):
+        op(nm, "v", lambda q: q.quantize_mx(c, s, a), r, w)
 
     def mm(bank, n_, lc, ls, rc, rs_, r):
-        op("t", lambda q: q.matmul_mx(T.ps[:, 512 * bank:512 * bank + n_], lc, ls, rc, rs_, True, True), r, ["b%d" % bank])
+        op(None, "t", lambda q: q.matmul_mx(T.ps[:, 512 * bank:512 * bank + n_], lc, ls, rc, rs_, True, True), r, ["b%d" % bank])
 
     def iota(out, pat, base, cmul, w, flt=False):
         if flt:
-            op("g", lambda q: q.iota(out, pat, base, cmul, allow_small_or_imprecise_dtypes=True), (), w)
+            op(None, "g", lambda q: q.iota(out, pat, base, cmul, allow_small_or_imprecise_dtypes=True), (), w)
         else:
-            op("g", lambda q: q.iota(out, pat, base, cmul), (), w)
+            op(None, "g", lambda q: q.iota(out, pat, base, cmul), (), w)
 
     def bank(b, n_):
         return T.ps[:, 512 * b:512 * b + n_]
@@ -192,14 +220,15 @@ def rank_program(g, core, T, topo):
 
     u32 = dt.uint32
     vv, cs, rho = 0, 256, 512
-    dma("s", T.xin[:], T.x[:], (), ["xin"])
-    dma("a", T.uin[:], T.u[:], (), ["uin"])
-    dma("s", T.tin[:], T.tri[:], ["uin"], ["tin"])
-    dma("s", T.wq[:].bitcast(dt.uint8), T.wc[:], ["xin"], ["wq"])
-    dma("s", T.wp[:], T.ws[:], (), ["wp"])
+    dma(None, "s", T.xin[:], T.x[:], (), ["xin"])
+    dma(None, "a", T.uin[:], T.u[:], (), ["uin"])
+    dma(None, "s", T.tin[:], T.tri[:], ["uin"], ["tin"])
+    dma(None, "s", T.wq[:].bitcast(dt.uint8), T.wc[:], ["xin"], ["wq"])
+    dma(None, "s", T.wp[:], T.ws[:], (), ["wp"])
+    dma(None, "s", T.vin[:], T.v[:], (), ["vin"])
     fill(T.ones[:], 1.0, ["ones"])
     iota(T.icol[:], [[16, 16]], 0, 0, ["icol"])
-    op("g", lambda q: q.affine_select(T.ident[:], T.ones[:], [[-1, 128]], A.is_equal, 0.0, 0, 1), ["ones"], ["ident"])
+    op(None, "g", lambda q: q.affine_select(T.ident[:], T.ones[:], [[-1, 128]], A.is_equal, 0.0, 0, 1), ["ones"], ["ident"])
     iota(T.ia[:, 0:16], [[1, 16]], 0, 16, ["ia0"])
     iota(T.ipart[:], [[0, 2]], 0, 1, ["ipart"])
     iota(T.ia[:, 16:32], [[16, 16]], 16, 16, ["ia1"])
@@ -207,13 +236,12 @@ def rank_program(g, core, T, topo):
     iota(T.yi[:], [[0, 16], [1, 16]], 0, 0, ["yi"], True)
     iota(T.targ[:], [[1, 11], [-1, 16]], 1, 0, ["targ"], True)
     iota(T.rkc[:, 0:16], [[-1, 16]], 14, 0, ["rkc0"], True)
-    iota(T.m32[:], [[0, 512]], -32, 0, ["m32"], True)
     iota(T.x2[:], [[0, 2], [1, 16]], 0, 0, ["x2"], True)
     iota(T.inid[:], [[33, 16]], -512, 0, ["inid"], True)
     iota(T.rkc[:, 16:32], [[1, 16]], 10, 0, ["rkc1"], True)
     iota(T.zz[:], [[0, 768]], 0, 0, ["zz", "cs", "rho"], True)
     iota(T.ze[:, 384:512], [[0, 128]], 0, 0, ["zep"], True)
-    dma("g", T.vin[:], T.v[:], (), ["vin"])
+    iota(T.d0[:, 0:1024:2], [[0, 256], [-1, 2]], 0, 0, ["d02"], True)
     fill(T.ebig[:], 0.0, ["ebig"])
     fill(T.keep[:], 1.0, ["keep"])
     fill(T.flip[:], 1.0, ["flip"])
@@ -222,28 +250,30 @@ def rank_program(g, core, T, topo):
     fill(T.rk[:, 255:256], 16.0, ["rkp"])
     fill(T.keep[:, 0:272:16], 0.0, ["keep"])
     fill(T.flip[:, 0:240:16], 0.0, ["flip"])
-    cp(T.lu[:], T.icol[:], ["icol"], ["lu"])
-    cp(T.ebig[:, 3:515:4], T.ident[:], ["ident"], ["ebig"])
+    cp(None, T.lu[:], T.icol[:], ["icol"], ["lu"])
+    cp(None, T.ebig[:, 3:515:4], T.ident[:], ["ident"], ["ebig"])
     fill(T.flip[:, 15:240:15], -1.0, ["flip"])
-    ts(T.ib[:, 0:16], T.ia[:, 0:16], 255, None, A.bitwise_and, None, ["ia0"], ["ib0"])
+    ts(None, T.ib[:, 0:16], T.ia[:, 0:16], 255, None, A.bitwise_and, None, ["ia0"], ["ib0"])
     for b in range(4):
-        quant(T.eq[:, 128 * b:128 * b + 128], T.ep[:, 128 * b:128 * b + 128], T.ebig[:, 3 - b:515 - b], ["ebig"], ["e%d" % b])
-    cp(T.lx[:], T.ib[:, 0:16], ["ib0"], ["lx"])
-    ts(T.ipm[:, 0:2], T.ipart[:], 15, None, A.bitwise_and, None, ["ipart"], ["ipm0"])
-    ts(T.ib[:, 16:48], T.ia[:, 16:48], 255, None, A.bitwise_and, None, ["ia1", "ia2"], ["ib1"])
-    quant(T.uq0[:], T.up0[:], T.uin[:], ["uin"], ["uq0"])
-    cp(T.pif[:], T.ipm[:, 0:1], ["ipm0"], ["pif"])
-    tt(T.ic[:, 0:16], T.ib[:, 16:32], T.icol[:], A.min, ["ib1", "icol"], ["ic0"])
-    cp(T.uq[:].bitcast(u32), T.uq0[:].bitcast(u32).indirect(T.lu[:, 0:8]), ["uq0", "lu"], ["uq"])
-    act(T.up[:], T.up0[:].indirect(T.lu[:, 0:8]), ["uq0", "lu"], ["up"])
-    quant(T.xq0[:], T.xp0[:], T.xin[:], ["xin"], ["xq0"])
-    tt(T.ic[:, 16:32], T.ib[:, 16:32], T.icol[:], A.max, ["ib1", "icol"], ["ic1"])
-    ts(T.msk[:], T.yi[:], T.pif[:], None, A.is_equal, None, ["yi", "pif"], ["msk"])
+        quant(None, T.eq[:, 128 * b:128 * b + 128], T.ep[:, 128 * b:128 * b + 128], T.ebig[:, 3 - b:515 - b], ["ebig"], ["e%d" % b])
+    cp(None, T.lx[:], T.ib[:, 0:16], ["ib0"], ["lx"])
+    ts(None, T.ipm[:, 0:2], T.ipart[:], 15, None, A.bitwise_and, None, ["ipart"], ["ipm0"])
+    ts(None, T.ib[:, 16:48], T.ia[:, 16:48], 255, None, A.bitwise_and, None, ["ia1", "ia2"], ["ib1"])
+    fill(T.c16[:], 1.0 / 16.0, ["c16"])
+    quant(None, T.uq0[:], T.up0[:], T.uin[:], ["uin"], ["uq0"])
+    cp(None, T.pif[:], T.ipm[:, 0:1], ["ipm0"], ["pif"])
+    tt(None, T.ic[:, 0:16], T.ib[:, 16:32], T.icol[:], A.min, ["ib1", "icol"], ["ic0"])
+    cp(None, T.uq[:].bitcast(u32), T.uq0[:].bitcast(u32).indirect(T.lu[:, 0:8]), ["uq0", "lu"], ["uq"])
+    act(None, T.up[:], T.up0[:].indirect(T.lu[:, 0:8]), ["uq0", "lu"], ["up"])
+    quant(None, T.xq0[:], T.xp0[:], T.xin[:], ["xin"], ["xq0"])
+    tt(None, T.ic[:, 16:32], T.ib[:, 16:32], T.icol[:], A.max, ["ib1", "icol"], ["ic1"])
+    ts(None, T.msk[:], T.yi[:], T.pif[:], None, A.is_equal, None, ["yi", "pif"], ["msk"])
     for k in range(2):
-        cp(T.xc0[:, 128 * k:128 * k + 128].bitcast(u32), T.xq0[:].bitcast(u32).indirect(T.lx[:, 8 * k:8 * k + 8]), ["xq0", "lx"], ["xc0%d" % k])
-        act(T.xs0[:, 128 * k:128 * k + 128], T.xp0[:].indirect(T.lx[:, 8 * k:8 * k + 8]), ["xq0", "lx"], ["xs0%d" % k])
-    ts(T.lcmp[:], T.ic[:], 15.0, None, A.add, None, ["ic0", "ic1"], ["lcmp"])
-    cp(T.linv[:], T.ib[:, 32:48], ["ib1"], ["linv"])
+        cp(None, T.xc0[:, 128 * k:128 * k + 128].bitcast(u32), T.xq0[:].bitcast(u32).indirect(T.lx[:, 8 * k:8 * k + 8]), ["xq0", "lx"], ["xc0%d" % k])
+        act(None, T.xs0[:, 128 * k:128 * k + 128], T.xp0[:].indirect(T.lx[:, 8 * k:8 * k + 8]), ["xq0", "lx"], ["xs0%d" % k])
+    ts(None, T.lcmp[:], T.ic[:], 15.0, None, A.add, None, ["ic0", "ic1"], ["lcmp"])
+    cp(None, T.linv[:], T.ib[:, 32:48], ["ib1"], ["linv"])
+    act(None, T.x2s[:], T.x2[:], ["x2"], ["x2s"], scale=1.0 / 512.0)
 
     def o_(j):
         return T.ob[:, 16 * j + 15:16 * j + 16]
@@ -251,82 +281,66 @@ def rank_program(g, core, T, topo):
     def plane(b):
         return T.hf[:, 256 * b:256 * b + 256]
 
-    def switch_u():
-        scan(T.u4[:], T.d0[:], T.d1[:], ["d01", "d02", "d03", "d10", "d11", "d12", "d13"], ["u4"])
-
-    def switch_copy():
-        cp(T.uu[:], T.u4[:, 3:1024:4], ["u4"], ["uu"])
-
-    def switch_new(k):
-        tt(T["tb%d" % k][:], T.u4[:].indirect(T.ltr[:]), T.uu[:], A.add, ["u4", "uu", "ltr"], ["tb%d" % k])
-
     for h in range(R):
+        now[0] = h
         xc, xs = T["xc%d" % h], T["xs%d" % h]
         kx = [["xc%d%d" % (h, k), "xs%d%d" % (h, k)] for k in range(2)]
-        tb = T["tb%d" % h]
-        ktb = "tb%d" % h
+        tb, ktb = T["tb%d" % h], "tb%d" % h
+        ub, un = T["ub%d" % (h % 2)], T["ub%d" % (1 - h % 2)]
+        ku, kn = four("u%d" % (h % 2)), four("u%d" % (1 - h % 2))
         zq, zp, qw, pw = T["zq%d" % h], T["zp%d" % h], T["qw%d" % h], T["pw%d" % h]
+        if h == 0:
+            ts("ltr", T.ltr[:], T.ib[:, 0:16], 4.0, 3.0, A.mult, A.add, ["ib0"], ["ltr"])
+            ts("ipm1", T.ipm[:, 2:4], T.ipart[:], 31, None, A.bitwise_and, None, ["ipart"], ["ipm1"])
+            cp("lhalf", T.lhalf[:], T.ipm[:, 2:4], ["ipm1"], ["lhalf"])
+            cp("tb0", T.tb0[:], T.tin[:], ["tin"], ["tb0"])
+            ts("uinit", ub[:, 3:1024:4], T.tb0[:], 0.5, LIFT, A.mult, A.add, ["tb0"], [ku[3]])
         for k in range(2):
             mm(k, 128, T.uq[:], T.up[:], xc[:, 128 * k:128 * k + 128], xs[:, 128 * k:128 * k + 128], ["uq", "up"] + kx[k])
         for b in range(4):
             mm(2 + b, 256, T.eq[:, 128 * b:128 * b + 128], T.ep[:, 128 * b:128 * b + 128], xc[:], xs[:], ["e%d" % b] + kx[0] + kx[1])
-        if h > 0:
-            switch_u()
-        tt(T.mb[:, 0:128], bank(0, 128), T.msk[:, 0:128], A.mult, ["msk"], ["mb0", "b0"])
-        tt(T.mb[:, 128:240], bank(1, 112), T.msk[:, 128:240], A.mult, ["msk"], ["mb1", "b1"])
-        if h > 0:
-            switch_copy()
+        halves = [(0, 128), (128, 240)]
+        for k, (a, z) in enumerate(halves):
+            tt("mb%d" % k, T.mb[:, a:z], bank(k, z - a), T.msk[:, a:z], A.mult, ["msk"], ["mb%d" % k, "b%d" % k])
+            scan("sc%d" % k, T.sc[:, a:z], T.keep[:, a:z], T.mb[:, a:z], ["keep", "mb%d" % k], ["sc%d" % k])
+        for b in range(4):
+            act("hf%d" % b, plane(b), bank(2 + b, 256), (), ["hf%d" % b, "b%d" % (2 + b)], scale=0.5)
+            act("wg%d" % b, T.wn[:, WN * b + 160:WN * b + WN], plane(b), ["hf%d" % b], ["wg%d" % b], scale=64.0)
+        act("g1a", T.g1[:, 0:128], T.sc[:, 0:128].indirect(T.lcmp[:, 0:8]), ["sc0", "lcmp"], ["g1a"])
+        act("g1b", T.g1[:, 128:240], T.sc[:, 0:240].indirect(T.lcmp[:, 8:15]), ["sc0", "sc1", "lcmp"], ["g1b"])
+        for k, (a, z) in enumerate(halves):
+            c = "ab"[k]
+            tt("cm" + c, T.cm[:, a:z], T.sc[:].indirect(T.lcmp[:, 16 + a // 16:16 + z // 16]), T.g1[:, a:z], A.is_le,
+               ["sc0", "sc1", "scp", "lcmp", "g1" + c], ["cm" + c])
+            scan("rk" + c, T.rk[:, a:z], T.flip[:, a:z], T.cm[:, a:z], ["flip", "cm" + c], ["rk" + c])
+        krk = ["rka", "rkb", "rkp"]
+        for c, a, z, s0, s1 in (("E", 0, 5, 0, 4), ("L", 5, 11, 4, 10)):
+            tt("nq" + c, T.nq[:, 16 * a:16 * z], T.rk[:].indirect(T.linv[:, 0:z - a]), T.targ[:, 16 * a:16 * z], A.not_equal, krk + ["linv", "targ"], ["nq" + c])
+            scan("ob" + c, T.ob[:, 16 * a:16 * z], T.nq[:, 16 * a:16 * z], T.keep[:, 16 * a + 1:16 * z + 1], ["nq" + c, "keep"], ["ob" + c])
+            scan("sx" + c, T.sx[:, a:z], T.c16[:, a:z], T.ob[:, 16 * a + 15:16 * z:16], ["c16", "ob" + c] + (["sxE"] if a else []), ["sx" + c],
+                 first=T.sx[:, a - 1:a] if a else 0.0)
+            ts("oidx" + c, T.oidx[:, s0:s1], T.sx[:, s0 + 1:s1 + 1], 16.0, -0.47, A.mult, A.add, ["sx" + c], ["oidx" + c])
+            ts("osec" + c, T.osec[:, s0:s1], T.ob[:, 16 * s0 + 31:16 * s1 + 16:16], 16.0, T.pif[:], A.mult, A.add, ["ob" + c, "pif"], ["osec" + c])
+            tt("lk" + c, T.lk[:, 16 * s0:16 * s1], tb[:].indirect(T.oidx[:, s0:s1]), T.msk[:, 16 * s0:16 * s1], A.mult, [ktb, "msk", "oidx" + c], ["lk" + c])
+            scan("ms" + c, T.ms[:, 16 * s0:16 * s1], T.keep[:, 16 * s0:16 * s1], T.lk[:, 16 * s0:16 * s1], ["keep", "lk" + c], ["ms" + c])
+            ts("oth" + c, T.othird[:, s0:s1], T.ms[:, 16 * s0 + 15:16 * s1:16], 16.0, T.pif[:], A.mult, A.add, ["ms" + c, "pif"], ["oth" + c])
+            for b in range(4):
+                act("a%s%d" % (c, b), T.aa[:, 160 * b + 16 * s0:160 * b + 16 * s1], plane(b).indirect(T.osec[:, s0:s1]), ["hf%d" % b, "osec" + c], ["a%s%d" % (c, b)])
+        tt("rr0", T.rr[:, 0:16], T.rk[:, 15:256:16], T.rkc[:, 0:16], A.add, krk + ["rkc0"], ["rr0"])
+        ts("rr1", T.rr[:, 16:32], T.rr[:, 0:16], -9.0, 30.0, A.add, A.mult, ["rr0"], ["rr1"])
+        tt("rr2", T.rr[:, 32:48], T.rr[:, 0:16], T.rr[:, 16:32], A.max, ["rr0", "rr1"], ["rr2"])
+        tt("rr3", T.rr[:, 48:64], T.rr[:, 32:48], T.rkc[:, 16:32], A.min, ["rr2", "rkc1"], ["rr"])
+        if h < R - 1:
+            ts("onew", T.onew[:], T.rr[:, 48:64], 16.0, T.pif[:], A.mult, A.add, ["rr", "pif"], ["onew"])
         else:
-            ts(T.ltr[:], T.ib[:, 0:16], 4.0, 3.0, A.mult, A.add, ["ib0"], ["ltr"])
-        act(plane(0), bank(2, 256), (), ["hf0", "b2"], scale=0.5)
-        scan(T.sc[:, 0:240], T.keep[:, 0:240], T.mb[:], ["keep", "mb0", "mb1"], ["sc"])
-        if h == 0:
-            ts(T.ipm[:, 2:4], T.ipart[:], 31, None, A.bitwise_and, None, ["ipart"], ["ipm1"])
-        cp(T.g1[:, 0:128], T.sc[:].indirect(T.lcmp[:, 16:24]), ["sc", "scp", "lcmp"], ["g1a"])
-        act(T.g1[:, 128:240], T.sc[:].indirect(T.lcmp[:, 24:31]), ["sc", "scp", "lcmp"], ["g1b"])
-        if h == 0:
-            cp(T.lhalf[:], T.ipm[:, 2:4], ["ipm1"], ["lhalf"])
-        tt(T.cm[:], T.sc[:].indirect(T.lcmp[:, 0:15]), T.g1[:], A.is_ge, ["sc", "scp", "lcmp", "g1a", "g1b"], ["cm"])
-        for b in range(1, 4):
-            act(plane(b), bank(2 + b, 256), (), ["hf%d" % b, "b%d" % (2 + b)], scale=0.5)
-        for b in range(2):
-            act(T.wn[:, WN * b + 160:WN * b + WN], plane(b), ["hf%d" % b], ["wg%d" % b], scale=64.0)
-        if h == 0:
-            cp(T.tb0[:], T.tin[:], ["tin"], ["tb0"])
-        else:
-            switch_new(h)
-        scan(T.rk[:, 0:240], T.flip[:], T.cm[:], ["flip", "cm"], ["rk"])
-        tt(T.nq[:], T.rk[:].indirect(T.linv[:, 0:11]), T.targ[:], A.not_equal, ["rk", "rkp", "linv", "targ"], ["nq"])
-        tt(T.rr[:, 0:16], T.rk[:, 15:256:16], T.rkc[:, 0:16], A.add, ["rk", "rkp", "rkc0"], ["rr0"])
-        scan(T.ob[:], T.nq[:], T.keep[:, 1:177], ["nq", "keep"], ["ob"])
-        tt(T.sg[:, 15:256:16], T.nq[:, 16:32], T.nq[:, 0:16], A.subtract, ["nq"], ["sg"])
-        ts(T.rr[:, 16:32], T.rr[:, 0:16], -9.0, 30.0, A.add, A.mult, ["rr0"], ["rr1"])
-        ts(T.o16[:, 0:10], T.ob[:, 15:160:16], 16.0, None, A.mult, None, ["ob"], ["o16"])
-        ts(T.osec[:, 0:10], T.ob[:, 31:176:16], 16.0, T.pif[:], A.mult, A.add, ["ob", "pif"], ["osec"])
+            for k in range(2):
+                ts("of2%d" % k, T.of2[:, 16 * k:16 * k + 16], T.rr[:, 48:64], 16.0, T.pif[:], A.mult, A.add, ["rr", "pif"], ["of2%d" % k])
+            op("oft", "v", lambda q: q.transpose(T.oft[:], T.of2[:]), ["of20", "of21"], ["oft"])
+            cp("onewT", T.onew[:], T.oft[:].indirect(T.lhalf[:, 0:1]), ["oft", "lhalf"], ["onew"])
         for b in range(4):
-            act(T.aa[:, 160 * b:160 * b + 64], plane(b).indirect(T.osec[:, 0:4]), ["hf%d" % b, "osec"], ["aa0%d" % b])
-        for b in range(4):
-            act(T.aa[:, 160 * b + 64:160 * b + 160], plane(b).indirect(T.osec[:, 4:10]), ["hf%d" % b, "osec"], ["aa1%d" % b])
-        ts(T.nn[:, 0:256], tb[:], o_(0), None, A.not_equal, None, [ktb, "ob"], ["nn0"])
-        tt(T.o16[:, 16:26], T.o16[:, 0:10], T.ob[:, 31:176:16], A.add, ["ob", "o16"], ["o17"])
-        ts(T.nn[:, 256:512], tb[:], o_(1), None, A.not_equal, None, [ktb, "ob"], ["nn1"])
-        ts(T.sh[:, 0:1], o_(3), o_(2), -32.0, A.subtract, A.mult, ["ob"], ["sm0"])
-        cp(T.oidx[:, 0:10], T.o16[:, 16:26], ["o17"], ["oidx"])
-        scan(T.rs[:], T.nn[:], T.m32[:], ["nn0", "nn1", "m32"], ["rs"])
-        tt(T.lk[:], tb[:].indirect(T.oidx[:, 0:10]), T.msk[:, 0:160], A.mult, [ktb, "msk", "oidx"], ["lk"])
-        tt(T.rin[:], T.rs[:, 15:512:16], T.x2[:], A.add, ["rs", "x2"], ["rin"])
-        ts(T.sm[:, 1:2], o_(2), -32.0, 512.0, A.mult, A.add, ["ob"], ["sm1"])
-        scan(T.ms[:], T.keep[:, 0:160], T.lk[:], ["keep", "lk"], ["ms"])
-        ts(T.sm[:, 3:4], o_(1), o_(0), 0.5, A.subtract, A.mult, ["ob"], ["sm3"])
-        tt(T.rr[:, 32:48], T.rr[:, 0:16], T.rr[:, 16:32], A.max, ["rr0", "rr1"], ["rr2"])
-        ts(T.othird[:, 0:10], T.ms[:, 15:160:16], 16.0, T.pif[:], A.mult, A.add, ["ms", "pif"], ["oth"])
-        ts(T.sm[:, 2:3], T.ms[:, 15:16], o_(2), T.sh[:, 0:1], A.is_equal, A.mult, ["ms", "ob", "sm0"], ["sm2"])
-        tt(T.zz[:, rho:rho + 256:16], T.rin[:, 16:32], T.rin[:, 0:16], A.subtract, ["rin"], ["rho"])
-        for b in range(4):
-            tt(T.zl[:, b:256:4], plane(b).indirect(T.othird[:, 0:4]), T.aa[:, 160 * b:160 * b + 64], A.add,
-               ["hf%d" % b, "oth", "aa0%d" % b], ["zl%d" % b])
-        tt(T.rr[:, 48:64], T.rr[:, 32:48], T.rkc[:, 16:32], A.min, ["rr2", "rkc1"], ["rr"])
-        quant(zq[:], zp[:], T.zl[:], four("zl") + ["zlp"], ["zq%d" % h])
+            tt("zl%d" % b, T.zl[:, b:256:4], plane(b).indirect(T.othird[:, 0:4]), T.aa[:, 160 * b:160 * b + 64], A.add,
+               ["hf%d" % b, "othE", "aE%d" % b], ["zl%d" % b])
+        quant("qz", zq[:], zp[:], T.zl[:], four("zl") + ["zlp"], ["zq%d" % h])
         for part in range(2):
             rid, pid = topo.addr(to[part], core)
             es = topo.engines(core, to[part])
@@ -337,86 +351,76 @@ def rank_program(g, core, T, topo):
             else:
                 src = zp[:, 0:64]
                 dst = pw[:, 0:64] if direct else T["rp%d" % h][:]
-            op("g", lambda q, dst=dst, src=src, pid=pid, rid=rid, m=_mask(es), s=T.sem["arr%d" % h]: q.remote_dma(dst, src, s, T.sem.sent, pid, rid, m),
+            op(None, "g", lambda q, dst=dst, src=src, pid=pid, rid=rid, m=_mask(es), s=T.sem["arr%d" % h]: q.remote_dma(dst, src, s, T.sem.sent, pid, rid, m),
                ["zq%d" % h], (), "remote")
-        op(None, None, (), ["arr%d" % h], "ext", "arr%d" % h, n_arr)
-        if h == 0:
-            iota(T.d0[:, 0:1024:2], [[0, 256], [-1, 2]], 0, 0, ["d02"], True)
-        act(T.kb[:, 0:1], T.sm[:, 2:3], ["sm1", "sm2"], ["kb0"], AF.Identity, bias=T.sm[:, 1:2])
-        steps = [(0, None)] + [(max(s - 2, 0), ((s + 1) // 2 + s) % 2) for s in range(1, 12)]
-        for s0 in range(0, 12, 2):
-            for s in (s0, s0 + 1):
-                fr, row = steps[s]
-                src = T.inid[:] if row is None else T.rin[:, 16 * row:16 * row + 16]
-                act(T.tw[:, 16 * s:16 * s + 16], src, ["rin", "inid", "kb%d" % fr], ["tw%d" % s], AF.Abs, bias=T.kb[:, fr:fr + 1])
-            for s in (s0, s0 + 1):
-                kw = {"accum_out": T.kb[:, s:s + 1]} if 0 < s < 10 else {}
-                act(T.zz[:, vv + s:vv + 256:16], T.tw[:, 16 * s:16 * s + 16], ["tw%d" % s, "zz"], ["vv%d" % s] + (["kb%d" % s] if kw else []),
-                    AF.Relu, bias=512.0, scale=-32.0, **kw)
-            if s0 in (0, 2):
-                b = 2 + s0 // 2
-                act(T.wn[:, WN * b + 160:WN * b + WN], plane(b), ["hf%d" % b], ["wg%d" % b], scale=64.0)
-            elif s0 == 4:
-                act(T.z32[:, 0:256], T.zl[:, 0:256], four("zl"), ["z320"], scale=32.0)
+        op(None, None, None, (), ["arr%d" % h], "ext", "arr%d" % h, n_arr)
+        act("z32l", T.z32[:, 0:256], T.zl[:, 0:256], four("zl"), ["z320"], scale=32.0)
         for b in range(4):
-            tt(T.ze[:, b:384:4], plane(b).indirect(T.othird[:, 4:10]), T.aa[:, 160 * b + 64:160 * b + 160], A.add,
-               ["hf%d" % b, "oth", "aa1%d" % b], ["ze%d" % b])
-        scan(T.d1[:, 0:1024:4], T.keep[:, 0:256], T.zz[:, rho:rho + 256], ["keep", "rho"], ["d10"])
-        quant(qw[:, 64:192], pw[:, 64:192], T.ze[:], four("ze") + ["zep"], ["qe%d" % h])
+            tt("ze%d" % b, T.ze[:, b:384:4], plane(b).indirect(T.othird[:, 4:10]), T.aa[:, 160 * b + 64:160 * b + 160], A.add,
+               ["hf%d" % b, "othL", "aL%d" % b], ["ze%d" % b])
+        quant("qe", qw[:, 64:192], pw[:, 64:192], T.ze[:], four("ze") + ["zep"], ["qe%d" % h])
         for b in range(4):
             mm(2 + b, 128, T.wq[:, 128 * b:128 * b + 128], T.wp[:, 128 * b:128 * b + 128], qw[:, 64:192], pw[:, 64:192], ["wq", "wp", "qe%d" % h])
-        ts(T.z32[:, 256:640], T.ze[:, 0:384], 32.0, None, A.mult, None, four("ze"), ["z321"])
-        ts(T.d1[:, 1:1024:4], T.nn[:, 0:256], T.sm[:, 3:4], None, A.mult, None, ["nn0", "sm3"], ["d11"])
-        if h < R - 1:
-            ts(T.onew[:], T.rr[:, 48:64], 16.0, T.pif[:], A.mult, A.add, ["rr", "pif"], ["onew"])
-        else:
-            for k in range(2):
-                ts(T.of2[:, 16 * k:16 * k + 16], T.rr[:, 48:64], 16.0, T.pif[:], A.mult, A.add, ["rr", "pif"], ["of2%d" % k])
+        ts("z32e", T.z32[:, 256:640], T.ze[:, 0:384], 32.0, None, A.mult, None, four("ze"), ["z321"])
         for b in range(4):
-            tt(T.wn[:, WN * b + 64:WN * b + 160], bank(2 + b, 96), T.z32[:, 256 + b:640:4], A.add, ["z321"], ["we%d" % b, "b%d" % (2 + b)])
-        if h == R - 1:
-            op("v", lambda q: q.transpose(T.oft[:], T.of2[:]), ["of20", "of21"], ["oft"])
-        ts(T.d1[:, 2:1024:4], T.nn[:, 256:512], T.sm[:, 3:4], None, A.mult, None, ["nn1", "sm3"], ["d12"])
+            tt("we%d" % b, T.wn[:, WN * b + 64:WN * b + 160], bank(2 + b, 96), T.z32[:, 256 + b:640:4], A.add, ["z321"], ["we%d" % b, "b%d" % (2 + b)])
         if h == 1:
-            quant(T.vq[:], T.vp[:], T.vin[:], ["vin"], ["vq"])
-        if h == R - 1:
-            cp(T.onew[:], T.oft[:].indirect(T.lhalf[:, 0:1]), ["oft", "lhalf"], ["onew"])
-        ts(T.d1[:, 3:1024:4], tb[:], 0.5, None, A.mult, None, [ktb], ["d13"])
+            quant("vq", T.vq[:], T.vp[:], T.vin[:], ["vin"], ["vq"])
+        tt("sg", T.sg[:, 15:256:16], T.nq[:, 16:32], T.nq[:, 0:16], A.subtract, ["nqE"], ["sg"])
+        ts("sig", T.sm[:, 3:4], o_(1), o_(0), 0.5, A.is_gt, A.subtract, ["obE"], ["sig"])
+        act("dab", T.sh[:, 1:2], o_(0), ["obE"], ["dab"], AF.Abs, scale=-1.0, bias=o_(1))
+        act("s64", T.sm[:, 5:6], T.sm[:, 3:4], ["sig"], ["s64"], scale=-64.0)
+        for k in range(2):
+            ts("n%d" % k, ub[:, 1 + k:1024:4], tb[:], o_(k), T.sh[:, 1:2], A.not_equal, A.mult, [ktb, "obE", "dab"], [ku[1 + k]])
+            scan("rs%d" % k, T.rs[:, 256 * k:256 * k + 256], ub[:, 1 + k:1024:4], T.c16[:], [ku[1 + k], "c16"], ["rs%d" % k], A.min)
+        tt("rin", T.rin[:], T.x2s[:], T.rs[:, 15:512:16], A.subtract, ["rs0", "rs1", "x2s"], ["rin"])
+        tt("rho", T.zz[:, rho:rho + 256:16], T.rin[:, 16:32], T.rin[:, 0:16], A.subtract, ["rin"], ["rho"])
+        scan("d10", ub[:, 0:1024:4], T.keep[:, 0:256], T.zz[:, rho:rho + 256], ["keep", "rho"], [ku[0]])
+        act("d01", T.d0[:, 1:1024:4], T.sg[:].indirect(T.linv[:, 0:16]), ["sg", "linv", "s64"], ["d01"], scale=T.sm[:, 5:6])
+        act("t23", T.sm[:, 0:2], T.ob[:, 47:64:16], ["obE"], ["t23"], AF.Identity, scale=-32.0, bias=512.0)
+        act("sh", T.sh[:, 0:1], T.sm[:, 0:1], ["t23"], ["sh"], AF.Identity, scale=-1.0, bias=T.sm[:, 1:2])
+        ts("sm2", T.sm[:, 2:3], T.ms[:, 15:16], o_(2), T.sh[:, 0:1], A.is_equal, A.mult, ["msE", "obE", "sh"], ["sm2"])
+        act("kb0", T.kb[:, 0:1], T.sm[:, 2:3], ["t23", "sm2"], ["kb0"], AF.Identity, bias=T.sm[:, 0:1])
+        steps = [(0, None)] + [(max(s - 2, 0), ((s + 1) // 2 + s) % 2) for s in range(1, 12)]
+        for s, (fr, row) in enumerate(steps):
+            src, by = (T.inid[:], 1.0) if row is None else (T.rin[:, 16 * row:16 * row + 16], 512.0)
+            act("A%d" % s, T.tw[:, 16 * s:16 * s + 16], src, ["inid" if row is None else "rin", "kb%d" % fr], ["tw%d" % s], AF.Abs, bias=T.kb[:, fr:fr + 1], scale=by)
+            kw = {"accum_out": T.kb[:, s:s + 1]} if 0 < s < 10 else {}
+            act("B%d" % s, T.zz[:, vv + s:vv + 256:16], T.tw[:, 16 * s:16 * s + 16], ["tw%d" % s, "zz"], ["vv%d" % s] + (["kb%d" % s] if kw else []),
+                AF.Relu, bias=512.0, scale=-32.0, **kw)
+        scan("vs", T.vs[:], T.keep[:, 0:256], T.zz[:, vv:vv + 256], ["keep", "zz"] + ["vv%d" % s for s in range(12)], ["vs"])
+        ts("cs", T.zz[:, cs:cs + 256:16], T.vs[:, 15:256:16], 0.0, T.sm[:, 3:4], A.is_gt, A.mult, ["vs", "sig"], ["cs"])
+        scan("d03", T.d0[:, 3:1024:4], T.keep[:, 0:256], T.zz[:, cs:cs + 256], ["keep", "cs"], ["d03"])
+        scan("u", un[:], T.d0[:], ub[:], ["d01", "d02", "d03"] + ku, kn)
+        act("ut", T.ut[:], un[:].indirect(T.ltr[:]), kn + ["ltr"], ["ut"], AF.Identity, bias=-2.0 * LIFT)
+        scan("add", T["tb%d" % (h + 1)][:], un[:, 3:1024:4], T.ut[:], [kn[3], "ut"], ["tb%d" % (h + 1)], A.max)
         lb = [6, 7, 0, 1]
         for b in range(4):
             mm(lb[b], 128, T.wq[:, 128 * b:128 * b + 128], T.wp[:, 128 * b:128 * b + 128], qw[:, 0:128], pw[:, 0:128], ["wq", "wp", "qe%d" % h, "arr%d" % h])
         for b in range(4):
-            tt(T.wn[:, WN * b:WN * b + 64], bank(lb[b], 64), T.z32[:, b:256:4], A.add, ["z320"], ["wl%d" % b, "b%d" % lb[b]])
-        scan(T.vs[:], T.keep[:, 0:256], T.zz[:, vv:vv + 256], ["keep", "zz"] + ["vv%d" % s for s in range(12)], ["vs"])
+            tt("wl%d" % b, T.wn[:, WN * b:WN * b + 64], bank(lb[b], 64), T.z32[:, b:256:4], A.add, ["z320"], ["wl%d" % b, "b%d" % lb[b]])
         for b in range(4):
             win = T.wn[:, WN * b:WN * b + WN].indirect(T.onew[:])
             rd = ["wl%d" % b, "we%d" % b, "wg%d" % b, "onew"]
             if b < 2:
-                act(T.xn[:, b:1024:4], win, rd, ["xn%d" % b], scale=0.03125)
+                act("xn%d" % b, T.xn[:, b:1024:4], win, rd, ["xn%d" % b], scale=0.03125)
             else:
-                ts(T.xn[:, b:1024:4], win, 0.03125, None, A.mult, None, rd, ["xn%d" % b])
-            if b == 2:
-                ts(T.zz[:, cs:cs + 256:16], T.vs[:, 15:256:16], 0.0, None, A.is_gt, None, ["vs"], ["cs"])
-        act(T.d0[:, 1:1024:4], T.sg[:].indirect(T.linv[:, 0:16]), ["sg", "linv"], ["d01"], scale=-1.0 / 32.0)
-        scan(T.d0[:, 3:1024:4], T.keep[:, 0:256], T.zz[:, cs:cs + 256], ["keep", "cs"], ["d03"])
+                ts("xn%d" % b, T.xn[:, b:1024:4], win, 0.03125, None, A.mult, None, rd, ["xn%d" % b])
         nc, ns = T["xc%d" % (h + 1)], T["xs%d" % (h + 1)]
         for k in range(2):
-            quant(nc[:, 128 * k:128 * k + 128], ns[:, 128 * k:128 * k + 128], T.xn[:, 512 * k:512 * k + 512],
+            quant("q%d" % k, nc[:, 128 * k:128 * k + 128], ns[:, 128 * k:128 * k + 128], T.xn[:, 512 * k:512 * k + 512],
                   four("xn"), ["xc%d%d" % (h + 1, k), "xs%d%d" % (h + 1, k)])
+    now[0] = R
     xc, xs = T["xc%d" % R], T["xs%d" % R]
     kx = [["xc%d%d" % (R, k), "xs%d%d" % (R, k)] for k in range(2)]
     for k in range(2):
         mm(2 + k, 128, T.vq[:], T.vp[:], xc[:, 128 * k:128 * k + 128], xs[:, 128 * k:128 * k + 128], ["vq"] + kx[k])
-    switch_u()
-    dma("s", T.oc[:], xc[:].bitcast(dt.uint8), kx[0] + kx[1], ["oc"])
-    for k in range(2):
-        act(T.yo[:, 128 * k:128 * k + 128], bank(2 + k, 128), (), ["yo%d" % k, "b%d" % (2 + k)])
-    switch_copy()
-    switch_new(R)
+        cp("yo%d" % k, T.yo[:, 128 * k:128 * k + 128], bank(2 + k, 128), (), ["yo%d" % k, "b%d" % (2 + k)])
+    dma(None, "s", T.oc[:], xc[:].bitcast(dt.uint8), kx[0] + kx[1], ["oc"])
     for k in range(4):
-        dma("g" if k < 2 else "s", T.osc[4 * k:4 * k + 4, :], xs[32 * k:32 * k + 4, :], kx[0] + kx[1], ["os%d" % k])
-    dma("a", T.y[:], T.yo[:], ["yo0", "yo1"], ["y"])
-    dma("s", T.ot[:], T.tb3[:], ["tb%d" % R], ["ot"])
-    op("g", None, ["oc", "y", "ot"] + four("os"), ())
+        dma("os%d" % k, "s" if k < 2 else "a", T.osc[4 * k:4 * k + 4, :], xs[32 * k:32 * k + 4, :], kx[0] + kx[1], ["os%d" % k])
+    dma("y", "a", T.y[:], T.yo[:], ["yo0", "yo1"], ["y"])
+    dma(None, "s", T.ot[:], T.tb3[:], ["tb%d" % R], ["ot"])
+    op(None, "g", None, ["oc", "y", "ot"] + four("os"), ())
     _emit(g, T, ops)
     g.wait_ge(T.sem.sent, R * sum(len(topo.engines(core, c)) // 2 for c in to))

@@ -8,8 +8,8 @@ LIFT = 64.0
 _SB = {
     BF: dict(xin=1024, uin=512, vin=512, ones=128, ident=128, ebig=528, yi=256, msk=256, keep=272, flip=240, targ=176, c16=256,
              cm=240, rk=256, nq=176, ob=176, lk=160, ms=160, hf=1024, aa=640, zl=512, ze=512, z32=640, wn=4 * WN, xn=1024,
-             rs=512, sg=256, sh=2, zz=768, vs=256, d0=1024, ub0=1024, ub1=1024, ut=256, tb0=256, tb1=256, tb2=256),
-    F32: dict(pif=1, x2=32, x2s=32, inid=16, rkc=32, mb=240, sc=256, g1=240, sx=16, rr=64, of2=32, oft=32, rin=32, sm=8, kb=16, tw=192,
+             rs=512, sg=256, sh=4, zz=768, vs=256, d0=768, d2=512, sb=768, ub0=1552, ub1=1552, ut=256, tb0=256, tb1=256, tb2=256),
+    F32: dict(pif=1, x2=48, x2s=48, x2t=48, tv=80, rkc=48, mb=240, sc=256, g1=240, sx=16, rr=64, of2=32, oft=32, rin=64, sm=8, kb=16, tw=192,
               tb3=256, yo=256),
     I32: dict(tin=256, ia=48, ib=48, ic=32, icol=16, ipart=2, ipm=4),
     U16: dict(lx=16, lu=16, lcmp=32, linv=16, ltr=16, lhalf=2, osec=16, oidx=16, othird=16, onew=16),
@@ -27,17 +27,41 @@ SCRATCH["ps"] = ("psum", [128, 4096], F32)
 
 SEMAPHORES = ["cv", "ca", "ct", "cg", "sent"] + ["arr%d" % h for h in range(R)] + ["dm%d" % k for k in range(20)]
 
+GATHERS = [("xn0", "a", 0, 0, 16), ("xn1", "a", 1, 0, 16), ("xn5", "a", 3, 10, 16),
+           ("xn2", "v", 2, 0, 8), ("xn3", "v", 3, 0, 10), ("xn6", "v", 2, 8, 16)]
+
+LOWER = [("g1a", "a", 0, 4), ("g1v", "v", 4, 8), ("g1b", "a", 8, 15)]
+
 A = AluOpType
 AF = ActivationFunctionType
 
 ORDER = {
-    "v": """vs- cs- mb0 mb1 d03- sc0 sc1 u- ltr tb0 cma cmb rka rkb ipm1 add- nqE nqL obE obL sxE osecE uinit oidxE n0 n1 lkE osecL rs1 msE rs0 sxL
-            othE sm2 rin oidxL zl0 zl1 zl2 zl3 lkL qz lhalf msL rr0 sig othL sg rr1 ze0 ze1 ze2 ze3 rho rr2 qe rr3 d10 z32e of20 of21 oft
-            we0 we1 onewT onew vq we2 we3 wl0 wl1 wl2 wl3 xn2 xn3 q0 q1""",
-    "a": """g1a g1b ut- hf0 hf1 hf2 dab t23 hf3 aE0 aE1 sh aE2 aE3 aL0 aL1 aL2 kb0 aL3 A1 wg0 B1 A2 A0 wg1 B2 A3 A4 B3 s64 A5 B0 B5 B4 A7 A6 B7
-            z32l A9 B6 wg2 B9 A8 wg3 A11 B8 xn0 xn1 A10 B11 B10 d01""",
+    "EVEN": {
+        "v": """ipm1 msk qx lhalf lcmp qu xc0 uc xc1 linv mb0 mb1 sc0 sc1 g1v tb0 cma cmb rka rkb vq add- nqE nqL obE obL ox0 ox1 ox2 ox3 osecE osecL
+                lkE n0 sxL msE n1 sig othE rs0 zl0 zl1 zl2 zl3 sg rs1 qz
+                kb0 rin2 oidxL rr0 tv1 lkL rho rr1 rin msL tv0 d10 othL tv2 rr2 ze0 ze1 ze2 rr3 ze3 of20 of21 qe onew z32e b3 we0 uinit oft we1 we2 vs we3
+                wl0 onewT cs wl2 wl1 d03 wl3 xn2 *u xn3 xn6 q0 q1 u""",
+        "a": """xs0 us xs1 g1a g1b hf0 wg0 hf1 hf2 t23 dab hf3 aE0 x2s aE1 aE2 wg1 aE3 aL0 x2t aL1 s64 sh aL2 d01
+                A1 A2 aL3 B1 B2 A3 A4 z32l B3 B4 A5 A6 A0 tv3 B5 B6 A7 A8 e3 B7 B8 f3 e4 B0 f4 wg2 wg3 xn0 xn1 xn5 ut""",
+    },
+    "HASTE": {
+        "v": """mb0 mb1 sc0 sc1 g1v add- cma cmb rka rkb nqE nqL obE sg obL ox0 ox1 ox2 ox3 sxL osecL osecE
+                lkE oidxL n1 msE lkL othE n0 msL zl0 zl1 zl2 zl3 othL sig qz
+                rs1 rs0 rr0 ze0 kb0 rin2 rr1 ze1 ze2 ze3 rin rr2 tv0 qe rr3 z32e vq onew rho
+                wl0 d10 wl2 tv1 wl1 wl3 xn2 xn3 xn6 q0 tv2 q1 b3""",
+        "a": """g1a g1b hf0 wg0 hf1 hf2 dab wg1 hf3 t23 aE0 sh aE1 aE2 x2t aE3 wg2 aL0 aL1 z32l aL2 s64 aL3
+                A1 A2 d01 B1 B2 wg3 A3 A4 A0 B3 B4 A5 A6 xn0 xn1 xn5 B5 B6 A7 A8 tv3 B0 B7 B8 e3 e4 f3 f4""",
+    },
+    "CATCH": {
+        "v": """mb0 mb1 sc0 sc1 g1v vs- cma cs- cmb d03- rka rkb u- nqE nqL obE sg rr0 obL osecE ox0 ox1 ox2 add- sig sxL osecL ox3 rr1 n1 tv0
+                lkE n0 oidxL rs1 msE rs0 lkL tv1 othE rin2 kb0 rr2 msL zl0 rin zl1 zl2 zl3 othL rho tv2 qz
+                rr3 ze0 ze1 ze2 of20 ze3 qe d10 z32e of21 b3 oft we0 we1 vs onewT we2 cs
+                wl0 we3 wl2 d03 wl1 xn2 wl3 u xn3 xn6 q0 q1""",
+        "a": """g1a g1b hf0 hf1 hf2 wg0 wg1 ut- dab t23 hf3 aE0 aE1 x2t aE2 aL0 aL1 sh s64 aE3 d01
+                A1 A2 aL2 B1 B2 aL3 A3 A4 B3 B4 tv3 A0 A5 A6 B5 B6 wg2 A7 A8 e3 B7 B8 f3 e4 B0 f4 z32l wg3 xn0 xn1 xn5 ut""",
+    },
+    "TAIL": {"v": "add- yo0 yo1", "a": "os2 os3 ot y"},
 }
-TAIL = {"v": "vs- cs- d03- u- yo0 yo1 add-", "a": "os2 os3 ut- y"}
 
 
 def _mask(es):
@@ -52,24 +76,26 @@ def _relays(src, dst, group, topo):
     return sorted(cs, key=lambda c: (topo.die(c) != topo.die(src), c))[:2]
 
 
-def _queues(ops):
+def _queues(ops, plan):
     at = {(o["h"], o["name"]): i for i, o in enumerate(ops) if o["name"]}
     qs = {}
     for e in ("v", "a", "t", "g", "s", None):
-        if e not in ORDER:
+        if e not in ("v", "a"):
             qs[e] = [i for i, o in enumerate(ops) if o["e"] == e]
             continue
         qs[e] = [i for i, o in enumerate(ops) if o["e"] == e and not o["name"]]
         for h in range(R + 1):
-            for w in (ORDER[e] if h < R else TAIL[e]).split():
-                k = (h - 1, w[:-1]) if w.endswith("-") else (h, w)
+            for w in ORDER[plan[h]][e].split():
+                if w[0] == "*" and h != R - 1:
+                    continue
+                k = (h - 1, w[:-1]) if w.endswith("-") else (h, w.lstrip("*"))
                 if k in at and at[k] not in qs[e]:
                     qs[e].append(at[k])
         assert sorted(qs[e]) == [i for i, o in enumerate(ops) if o["e"] == e]
     return qs
 
 
-def _emit(g, T, ops):
+def _emit(g, T, ops, plan):
     q = {"v": g.vector, "a": g.scalar, "t": g.tensor, "g": g, "s": g.sync}
     cs = {"v": "cv", "a": "ca", "t": "ct", "g": "cg"}
     lastw, readers, deps = {}, {}, []
@@ -83,7 +109,7 @@ def _emit(g, T, ops):
         for k in o["w"]:
             lastw[k] = i
             readers[k] = []
-    qs = _queues(ops)
+    qs = _queues(ops, plan)
     pos = {i: n for e in qs for n, i in enumerate(qs[e])}
     known = {e: ({}, set()) for e in q}
     snap = {i: ({}, set()) for i in qs[None]}
@@ -168,6 +194,8 @@ def rank_program(g, core, T, topo):
     else:
         n_arr = sum(len(topo.engines(c, core)) for c in _relays(prv, core, cores, topo))
 
+    late = [int((h % 2 == 0) != topo.may_write(prv, core)) for h in range(R)]
+
     ops = []
     ndma = [0]
     now = [0]
@@ -221,59 +249,66 @@ def rank_program(g, core, T, topo):
     u32 = dt.uint32
     vv, cs, rho = 0, 256, 512
     dma(None, "s", T.xin[:], T.x[:], (), ["xin"])
-    dma(None, "a", T.uin[:], T.u[:], (), ["uin"])
-    dma(None, "s", T.tin[:], T.tri[:], ["uin"], ["tin"])
-    dma(None, "s", T.wq[:].bitcast(dt.uint8), T.wc[:], ["xin"], ["wq"])
+    dma(None, "s", T.uin[:], T.u[:], (), ["uin"])
+    dma(None, "s", T.tin[:], T.tri[:], ["xin"], ["tin"])
+    dma(None, "s", T.wq[:].bitcast(dt.uint8), T.wc[:], (), ["wq"])
     dma(None, "s", T.wp[:], T.ws[:], (), ["wp"])
     dma(None, "s", T.vin[:], T.v[:], (), ["vin"])
     fill(T.ones[:], 1.0, ["ones"])
     iota(T.icol[:], [[16, 16]], 0, 0, ["icol"])
-    op(None, "g", lambda q: q.affine_select(T.ident[:], T.ones[:], [[-1, 128]], A.is_equal, 0.0, 0, 1), ["ones"], ["ident"])
     iota(T.ia[:, 0:16], [[1, 16]], 0, 16, ["ia0"])
+    op(None, "g", lambda q: q.affine_select(T.ident[:], T.ones[:], [[-1, 128]], A.is_equal, 0.0, 0, 1), ["ones"], ["ident"])
     iota(T.ipart[:], [[0, 2]], 0, 1, ["ipart"])
     iota(T.ia[:, 16:32], [[16, 16]], 16, 16, ["ia1"])
     iota(T.ia[:, 32:48], [[0, 16]], 2303, -16, ["ia2"])
     iota(T.yi[:], [[0, 16], [1, 16]], 0, 0, ["yi"], True)
     iota(T.targ[:], [[1, 11], [-1, 16]], 1, 0, ["targ"], True)
     iota(T.rkc[:, 0:16], [[-1, 16]], 14, 0, ["rkc0"], True)
-    iota(T.x2[:], [[0, 2], [1, 16]], 0, 0, ["x2"], True)
-    iota(T.inid[:], [[33, 16]], -512, 0, ["inid"], True)
+    iota(T.x2[:, 0:32], [[0, 2], [1, 16]], 0, 0, ["x2"], True)
+    iota(T.x2[:, 32:48], [[33, 16]], -512, 0, ["inid"], True)
     iota(T.rkc[:, 16:32], [[1, 16]], 10, 0, ["rkc1"], True)
-    iota(T.zz[:], [[0, 768]], 0, 0, ["zz", "cs", "rho"], True)
+    iota(T.rkc[:, 32:48], [[-1, 16]], 16, 0, ["rkc2"], True)
     iota(T.ze[:, 384:512], [[0, 128]], 0, 0, ["zep"], True)
-    iota(T.d0[:, 0:1024:2], [[0, 256], [-1, 2]], 0, 0, ["d02"], True)
+    iota(T.d0[:, 0:768:3], [[0, 256]], 0, 0, ["d00"], True)
+    iota(T.d0[:, 2:768:3], [[0, 256]], -1, 0, ["d02"], True)
+    iota(T.d2[:, 0:512:2], [[0, 256]], 0, 0, ["d20"], True)
+    fill(T.zz[:, 0:256], 0.0, ["zz"])
     fill(T.ebig[:], 0.0, ["ebig"])
+    for out, c, w in ((T.zz[:, cs:cs + 256], 0.0, "cs"), (T.zz[:, rho:rho + 256], 0.0, "rho"), (T.zl[:, 256:512], 0.0, "zlp"), (T.c16[:], 1.0 / 16.0, "c16")):
+        act(None, out, T.zz[:, 0:256], ["zz"], [w], AF.Identity, bias=c)
     fill(T.keep[:], 1.0, ["keep"])
     fill(T.flip[:], 1.0, ["flip"])
-    fill(T.zl[:, 256:512], 0.0, ["zlp"])
-    fill(T.sc[:, 255:256], -1.0e29, ["scp"])
-    fill(T.rk[:, 255:256], 16.0, ["rkp"])
+    cp(None, T.lu[:], T.icol[:], ["icol"], ["lu"])
+    ts(None, T.ib[:, 0:16], T.ia[:, 0:16], 255, None, A.bitwise_and, None, ["ia0"], ["ib0"])
     fill(T.keep[:, 0:272:16], 0.0, ["keep"])
     fill(T.flip[:, 0:240:16], 0.0, ["flip"])
-    cp(None, T.lu[:], T.icol[:], ["icol"], ["lu"])
+    fill(T.sc[:, 255:256], -1.0e29, ["scp"])
+    cp(None, T.lx[:], T.ib[:, 0:16], ["ib0"], ["lx"])
     cp(None, T.ebig[:, 3:515:4], T.ident[:], ["ident"], ["ebig"])
     fill(T.flip[:, 15:240:15], -1.0, ["flip"])
-    ts(None, T.ib[:, 0:16], T.ia[:, 0:16], 255, None, A.bitwise_and, None, ["ia0"], ["ib0"])
+    ts(None, T.ipm[:, 0:2], T.ipart[:], 15, None, A.bitwise_and, None, ["ipart"], ["ipm0"])
+    fill(T.rk[:, 255:256], 16.0, ["rkp"])
+    ts(None, T.ltr[:], T.ib[:, 0:16], 6.0, 7.0, A.mult, A.add, ["ib0"], ["ltr"])
     for b in range(4):
         quant(None, T.eq[:, 128 * b:128 * b + 128], T.ep[:, 128 * b:128 * b + 128], T.ebig[:, 3 - b:515 - b], ["ebig"], ["e%d" % b])
-    cp(None, T.lx[:], T.ib[:, 0:16], ["ib0"], ["lx"])
-    ts(None, T.ipm[:, 0:2], T.ipart[:], 15, None, A.bitwise_and, None, ["ipart"], ["ipm0"])
-    ts(None, T.ib[:, 16:48], T.ia[:, 16:48], 255, None, A.bitwise_and, None, ["ia1", "ia2"], ["ib1"])
-    fill(T.c16[:], 1.0 / 16.0, ["c16"])
-    quant(None, T.uq0[:], T.up0[:], T.uin[:], ["uin"], ["uq0"])
+        if b == 1:
+            ts(None, T.ib[:, 16:48], T.ia[:, 16:48], 255, None, A.bitwise_and, None, ["ia1", "ia2"], ["ib1"])
     cp(None, T.pif[:], T.ipm[:, 0:1], ["ipm0"], ["pif"])
     tt(None, T.ic[:, 0:16], T.ib[:, 16:32], T.icol[:], A.min, ["ib1", "icol"], ["ic0"])
-    cp(None, T.uq[:].bitcast(u32), T.uq0[:].bitcast(u32).indirect(T.lu[:, 0:8]), ["uq0", "lu"], ["uq"])
-    act(None, T.up[:], T.up0[:].indirect(T.lu[:, 0:8]), ["uq0", "lu"], ["up"])
-    quant(None, T.xq0[:], T.xp0[:], T.xin[:], ["xin"], ["xq0"])
     tt(None, T.ic[:, 16:32], T.ib[:, 16:32], T.icol[:], A.max, ["ib1", "icol"], ["ic1"])
-    ts(None, T.msk[:], T.yi[:], T.pif[:], None, A.is_equal, None, ["yi", "pif"], ["msk"])
+    cp("linv", T.linv[:], T.ib[:, 32:48], ["ib1"], ["linv"])
+    ts("ipm1", T.ipm[:, 2:4], T.ipart[:], 31, None, A.bitwise_and, None, ["ipart"], ["ipm1"])
+    ts("msk", T.msk[:], T.yi[:], T.pif[:], None, A.is_equal, None, ["yi", "pif"], ["msk"])
+    ts("lcmp", T.lcmp[:], T.ic[:], 15.0, None, A.add, None, ["ic0", "ic1"], ["lcmp"])
+    cp("lhalf", T.lhalf[:], T.ipm[:, 2:4], ["ipm1"], ["lhalf"])
+    quant("qx", T.xq0[:], T.xp0[:], T.xin[:], ["xin"], ["xq0"])
+    quant("qu", T.uq0[:], T.up0[:], T.uin[:], ["uin"], ["uq0"])
     for k in range(2):
-        cp(None, T.xc0[:, 128 * k:128 * k + 128].bitcast(u32), T.xq0[:].bitcast(u32).indirect(T.lx[:, 8 * k:8 * k + 8]), ["xq0", "lx"], ["xc0%d" % k])
-        act(None, T.xs0[:, 128 * k:128 * k + 128], T.xp0[:].indirect(T.lx[:, 8 * k:8 * k + 8]), ["xq0", "lx"], ["xs0%d" % k])
-    ts(None, T.lcmp[:], T.ic[:], 15.0, None, A.add, None, ["ic0", "ic1"], ["lcmp"])
-    cp(None, T.linv[:], T.ib[:, 32:48], ["ib1"], ["linv"])
-    act(None, T.x2s[:], T.x2[:], ["x2"], ["x2s"], scale=1.0 / 512.0)
+        cp("xc%d" % k, T.xc0[:, 128 * k:128 * k + 128].bitcast(u32), T.xq0[:].bitcast(u32).indirect(T.lx[:, 8 * k:8 * k + 8]), ["xq0", "lx"], ["xc0%d" % k])
+        act("xs%d" % k, T.xs0[:, 128 * k:128 * k + 128], T.xp0[:].indirect(T.lx[:, 8 * k:8 * k + 8]), ["xq0", "lx"], ["xs0%d" % k])
+    cp("uc", T.uq[:].bitcast(u32), T.uq0[:].bitcast(u32).indirect(T.lu[:, 0:8]), ["uq0", "lu"], ["uq"])
+    act("us", T.up[:], T.up0[:].indirect(T.lu[:, 0:8]), ["uq0", "lu"], ["up"])
+    act("x2s", T.x2s[:], T.x2[:], ["x2", "inid"], ["x2s"], scale=1.0 / 512.0)
 
     def o_(j):
         return T.ob[:, 16 * j + 15:16 * j + 16]
@@ -287,14 +322,11 @@ def rank_program(g, core, T, topo):
         kx = [["xc%d%d" % (h, k), "xs%d%d" % (h, k)] for k in range(2)]
         tb, ktb = T["tb%d" % h], "tb%d" % h
         ub, un = T["ub%d" % (h % 2)], T["ub%d" % (1 - h % 2)]
-        ku, kn = four("u%d" % (h % 2)), four("u%d" % (1 - h % 2))
+        ku, kn, kb, kbn = "u%d" % (h % 2), "u%d" % (1 - h % 2), "bb%d" % (h % 2), "bb%d" % (1 - h % 2)
         zq, zp, qw, pw = T["zq%d" % h], T["zp%d" % h], T["qw%d" % h], T["pw%d" % h]
         if h == 0:
-            ts("ltr", T.ltr[:], T.ib[:, 0:16], 4.0, 3.0, A.mult, A.add, ["ib0"], ["ltr"])
-            ts("ipm1", T.ipm[:, 2:4], T.ipart[:], 31, None, A.bitwise_and, None, ["ipart"], ["ipm1"])
-            cp("lhalf", T.lhalf[:], T.ipm[:, 2:4], ["ipm1"], ["lhalf"])
             cp("tb0", T.tb0[:], T.tin[:], ["tin"], ["tb0"])
-            ts("uinit", ub[:, 3:1024:4], T.tb0[:], 0.5, LIFT, A.mult, A.add, ["tb0"], [ku[3]])
+            ts("uinit", ub[:, 7:1540:6], T.tb0[:], 0.5, LIFT, A.mult, A.add, ["tb0"], [ku])
         for k in range(2):
             mm(k, 128, T.uq[:], T.up[:], xc[:, 128 * k:128 * k + 128], xs[:, 128 * k:128 * k + 128], ["uq", "up"] + kx[k])
         for b in range(4):
@@ -306,22 +338,26 @@ def rank_program(g, core, T, topo):
         for b in range(4):
             act("hf%d" % b, plane(b), bank(2 + b, 256), (), ["hf%d" % b, "b%d" % (2 + b)], scale=0.5)
             act("wg%d" % b, T.wn[:, WN * b + 160:WN * b + WN], plane(b), ["hf%d" % b], ["wg%d" % b], scale=64.0)
-        act("g1a", T.g1[:, 0:128], T.sc[:, 0:128].indirect(T.lcmp[:, 0:8]), ["sc0", "lcmp"], ["g1a"])
-        act("g1b", T.g1[:, 128:240], T.sc[:, 0:240].indirect(T.lcmp[:, 8:15]), ["sc0", "sc1", "lcmp"], ["g1b"])
+        for nm, e, a, z in LOWER:
+            (act if e == "a" else cp)(nm, T.g1[:, 16 * a:16 * z], T.sc[:, 0:128 if a < 8 else 240].indirect(T.lcmp[:, a:z]), ["sc0", "lcmp"] + ["sc1"] * (a // 8), [nm])
         for k, (a, z) in enumerate(halves):
             c = "ab"[k]
             tt("cm" + c, T.cm[:, a:z], T.sc[:].indirect(T.lcmp[:, 16 + a // 16:16 + z // 16]), T.g1[:, a:z], A.is_le,
-               ["sc0", "sc1", "scp", "lcmp", "g1" + c], ["cm" + c])
+               ["sc0", "sc1", "scp", "lcmp"] + [nm for nm, e, a1, z1 in LOWER if a1 // 8 == k], ["cm" + c])
             scan("rk" + c, T.rk[:, a:z], T.flip[:, a:z], T.cm[:, a:z], ["flip", "cm" + c], ["rk" + c])
         krk = ["rka", "rkb", "rkp"]
         for c, a, z, s0, s1 in (("E", 0, 5, 0, 4), ("L", 5, 11, 4, 10)):
             tt("nq" + c, T.nq[:, 16 * a:16 * z], T.rk[:].indirect(T.linv[:, 0:z - a]), T.targ[:, 16 * a:16 * z], A.not_equal, krk + ["linv", "targ"], ["nq" + c])
             scan("ob" + c, T.ob[:, 16 * a:16 * z], T.nq[:, 16 * a:16 * z], T.keep[:, 16 * a + 1:16 * z + 1], ["nq" + c, "keep"], ["ob" + c])
-            scan("sx" + c, T.sx[:, a:z], T.c16[:, a:z], T.ob[:, 16 * a + 15:16 * z:16], ["c16", "ob" + c] + (["sxE"] if a else []), ["sx" + c],
-                 first=T.sx[:, a - 1:a] if a else 0.0)
-            ts("oidx" + c, T.oidx[:, s0:s1], T.sx[:, s0 + 1:s1 + 1], 16.0, -0.47, A.mult, A.add, ["sx" + c], ["oidx" + c])
+            if c == "E":
+                for j in range(4):
+                    ts("ox%d" % j, T.oidx[:, j:j + 1], o_(j), 16.0, o_(j + 1), A.mult, A.add, ["obE"], ["oidxE%d" % j])
+            else:
+                scan("sxL", T.sx[:, 0:7], T.c16[:, 0:7], T.ob[:, 79:176:16], ["c16", "obE", "obL"], ["sxL"])
+                ts("oidxL", T.oidx[:, 4:10], T.sx[:, 1:7], 16.0, -0.47, A.mult, A.add, ["sxL"], ["oidxL"])
             ts("osec" + c, T.osec[:, s0:s1], T.ob[:, 16 * s0 + 31:16 * s1 + 16:16], 16.0, T.pif[:], A.mult, A.add, ["ob" + c, "pif"], ["osec" + c])
-            tt("lk" + c, T.lk[:, 16 * s0:16 * s1], tb[:].indirect(T.oidx[:, s0:s1]), T.msk[:, 16 * s0:16 * s1], A.mult, [ktb, "msk", "oidx" + c], ["lk" + c])
+            tt("lk" + c, T.lk[:, 16 * s0:16 * s1], tb[:].indirect(T.oidx[:, s0:s1]), T.msk[:, 16 * s0:16 * s1], A.mult,
+               [ktb, "msk"] + (four("oidxE") if c == "E" else ["oidxL"]), ["lk" + c])
             scan("ms" + c, T.ms[:, 16 * s0:16 * s1], T.keep[:, 16 * s0:16 * s1], T.lk[:, 16 * s0:16 * s1], ["keep", "lk" + c], ["ms" + c])
             ts("oth" + c, T.othird[:, s0:s1], T.ms[:, 16 * s0 + 15:16 * s1:16], 16.0, T.pif[:], A.mult, A.add, ["ms" + c, "pif"], ["oth" + c])
             for b in range(4):
@@ -344,7 +380,7 @@ def rank_program(g, core, T, topo):
         for part in range(2):
             rid, pid = topo.addr(to[part], core)
             es = topo.engines(core, to[part])
-            es = es[:len(es) // 2] if part == 0 else es[len(es) // 2:]
+            es = es[part::2]
             if part == 0:
                 src = zq[:, 0:64].bitcast(dt.uint8)
                 dst = (qw[:, 0:64] if direct else T["rc%d" % h][:]).bitcast(dt.uint8)
@@ -359,57 +395,74 @@ def rank_program(g, core, T, topo):
             tt("ze%d" % b, T.ze[:, b:384:4], plane(b).indirect(T.othird[:, 4:10]), T.aa[:, 160 * b + 64:160 * b + 160], A.add,
                ["hf%d" % b, "othL", "aL%d" % b], ["ze%d" % b])
         quant("qe", qw[:, 64:192], pw[:, 64:192], T.ze[:], four("ze") + ["zep"], ["qe%d" % h])
-        for b in range(4):
+        together = 1 - late[h]
+        for b in range(0 if together else 4):
             mm(2 + b, 128, T.wq[:, 128 * b:128 * b + 128], T.wp[:, 128 * b:128 * b + 128], qw[:, 64:192], pw[:, 64:192], ["wq", "wp", "qe%d" % h])
         ts("z32e", T.z32[:, 256:640], T.ze[:, 0:384], 32.0, None, A.mult, None, four("ze"), ["z321"])
-        for b in range(4):
+        for b in range(0 if together else 4):
             tt("we%d" % b, T.wn[:, WN * b + 64:WN * b + 160], bank(2 + b, 96), T.z32[:, 256 + b:640:4], A.add, ["z321"], ["we%d" % b, "b%d" % (2 + b)])
         if h == 1:
             quant("vq", T.vq[:], T.vp[:], T.vin[:], ["vin"], ["vq"])
-        tt("sg", T.sg[:, 15:256:16], T.nq[:, 16:32], T.nq[:, 0:16], A.subtract, ["nqE"], ["sg"])
+        tt("sg", T.sg[:, 15:256:16], T.nq[:, 0:16], T.nq[:, 16:32], A.subtract, ["nqE"], ["sg"])
         ts("sig", T.sm[:, 3:4], o_(1), o_(0), 0.5, A.is_gt, A.subtract, ["obE"], ["sig"])
         act("dab", T.sh[:, 1:2], o_(0), ["obE"], ["dab"], AF.Abs, scale=-1.0, bias=o_(1))
-        act("s64", T.sm[:, 5:6], T.sm[:, 3:4], ["sig"], ["s64"], scale=-64.0)
+        act("s64", T.sm[:, 5:6], T.sm[:, 3:4], ["sig"], ["s64"], scale=64.0)
         for k in range(2):
-            ts("n%d" % k, ub[:, 1 + k:1024:4], tb[:], o_(k), T.sh[:, 1:2], A.not_equal, A.mult, [ktb, "obE", "dab"], [ku[1 + k]])
-            scan("rs%d" % k, T.rs[:, 256 * k:256 * k + 256], ub[:, 1 + k:1024:4], T.c16[:], [ku[1 + k], "c16"], ["rs%d" % k], A.min)
-        tt("rin", T.rin[:], T.x2s[:], T.rs[:, 15:512:16], A.subtract, ["rs0", "rs1", "x2s"], ["rin"])
-        tt("rho", T.zz[:, rho:rho + 256:16], T.rin[:, 16:32], T.rin[:, 0:16], A.subtract, ["rin"], ["rho"])
-        scan("d10", ub[:, 0:1024:4], T.keep[:, 0:256], T.zz[:, rho:rho + 256], ["keep", "rho"], [ku[0]])
-        act("d01", T.d0[:, 1:1024:4], T.sg[:].indirect(T.linv[:, 0:16]), ["sg", "linv", "s64"], ["d01"], scale=T.sm[:, 5:6])
-        act("t23", T.sm[:, 0:2], T.ob[:, 47:64:16], ["obE"], ["t23"], AF.Identity, scale=-32.0, bias=512.0)
+            ts("n%d" % k, T.sb[:, 1 + k:768:3], tb[:], o_(k), T.sh[:, 1:2], A.not_equal, A.mult, [ktb, "obE", "dab"], ["sb%d" % k])
+            scan("rs%d" % k, T.rs[:, 256 * k:256 * k + 256], T.sb[:, 1 + k:768:3], T.c16[:], ["sb%d" % k, "c16"], ["rs%d" % k], A.min)
+        tt("rin", T.rin[:, 0:32], T.x2s[:, 0:32], T.rs[:, 15:512:16], A.subtract, ["rs0", "rs1", "x2s"], ["rin"])
+        tt("rho", T.zz[:, rho:rho + 256:16], T.rs[:, 15:256:16], T.rs[:, 271:512:16], A.subtract, ["rs0", "rs1"], ["rho"])
+        scan("d10", T.sb[:, 0:768:3], T.keep[:, 0:256], T.zz[:, rho:rho + 256], ["keep", "rho"], ["sb2"])
+        act("d01", T.d0[:, 1:768:3], T.sg[:].indirect(T.linv[:, 0:16]), ["sg", "linv", "s64"], ["d01"], scale=T.sm[:, 5:6])
+        scan("b3", ub[:, 0:1536:2], T.d0[:], T.sb[:], ["d00", "d01", "d02", "sb0", "sb1", "sb2"], [kb])
+        act("t23", T.sm[:, 0:2], T.ob[:, 47:64:16], ["obE"], ["t23"], AF.Identity, scale=-1.0 / 16.0, bias=1.0)
         act("sh", T.sh[:, 0:1], T.sm[:, 0:1], ["t23"], ["sh"], AF.Identity, scale=-1.0, bias=T.sm[:, 1:2])
-        ts("sm2", T.sm[:, 2:3], T.ms[:, 15:16], o_(2), T.sh[:, 0:1], A.is_equal, A.mult, ["msE", "obE", "sh"], ["sm2"])
-        act("kb0", T.kb[:, 0:1], T.sm[:, 2:3], ["t23", "sm2"], ["kb0"], AF.Identity, bias=T.sm[:, 0:1])
-        steps = [(0, None)] + [(max(s - 2, 0), ((s + 1) // 2 + s) % 2) for s in range(1, 12)]
+        act("x2t", T.x2t[:], T.x2s[:], ["t23", "x2s"], ["x2t"], AF.Identity, bias=T.sm[:, 0:1])
+        tt("rin2", T.rin[:, 32:64], T.x2t[:, 0:32], T.rs[:, 15:512:16], A.subtract, ["rs0", "rs1", "x2t"], ["rin2"])
+        ts("kb0", T.kb[:, 0:1], T.ms[:, 15:16], o_(2), T.sh[:, 0:1], A.is_equal, A.mult, ["msE", "obE", "sh"], ["kb0"])
+        tt("tv0", T.tv[:, 0:16], T.rr[:, 0:16], T.rkc[:, 32:48], A.min, ["rr0", "rkc2"], ["tv0"])
+        ts("tv1", T.tv[:, 16:32], T.yi[:, 0:16], T.ms[:, 15:16], 16.0, A.not_equal, A.mult, ["yi", "msE"], ["tv1"])
+        tt("tv2", T.tv[:, 32:48], T.tv[:, 0:16], T.tv[:, 16:32], A.min, ["tv0", "tv1"], ["tv2"])
+        act("tv3", T.tv[:, 48:64], T.tv[:, 32:48], ["tv2"], ["tv3"], AF.Relu, bias=-1.0)
+        steps = [(0, None)] + [(max(s - 2, 0), ((s + 1) // 2 + s) % 2) for s in range(1, 9)]
         for s, (fr, row) in enumerate(steps):
-            src, by = (T.inid[:], 1.0) if row is None else (T.rin[:, 16 * row:16 * row + 16], 512.0)
-            act("A%d" % s, T.tw[:, 16 * s:16 * s + 16], src, ["inid" if row is None else "rin", "kb%d" % fr], ["tw%d" % s], AF.Abs, bias=T.kb[:, fr:fr + 1], scale=by)
+            if row is None:
+                src, ks = T.x2t[:, 32:48], "x2t"
+            else:
+                src, ks = (T.rin[:, 16 * row:16 * row + 16], "rin") if fr else (T.rin[:, 32 + 16 * row:48 + 16 * row], "rin2")
+            act("A%d" % s, T.tw[:, 16 * s:16 * s + 16], src, [ks, "kb%d" % fr], ["tw%d" % s], AF.Abs, bias=T.kb[:, fr:fr + 1])
             kw = {"accum_out": T.kb[:, s:s + 1]} if 0 < s < 10 else {}
             act("B%d" % s, T.zz[:, vv + s:vv + 256:16], T.tw[:, 16 * s:16 * s + 16], ["tw%d" % s, "zz"], ["vv%d" % s] + (["kb%d" % s] if kw else []),
-                AF.Relu, bias=512.0, scale=-32.0, **kw)
-        scan("vs", T.vs[:], T.keep[:, 0:256], T.zz[:, vv:vv + 256], ["keep", "zz"] + ["vv%d" % s for s in range(12)], ["vs"])
+                AF.Relu, bias=1.0, scale=-32.0, **kw)
+        act("e3", T.kb[:, 10:11], T.kb[:, 5:6], ["kb5", "kb6"], ["e3"], AF.Abs, scale=-1.0, bias=T.kb[:, 6:7])
+        act("f3", T.tv[:, 64:80], T.tv[:, 48:64], ["tv3", "e3"], ["f3"], AF.Identity, scale=T.kb[:, 10:11])
+        act("e4", T.kb[:, 11:12], T.kb[:, 7:8], ["kb7", "kb8"], ["e4"], AF.Abs, scale=-1.0, bias=T.kb[:, 8:9])
+        act("f4", T.zz[:, vv + 9:vv + 256:16], T.tv[:, 64:80], ["f3", "e4", "zz"], ["vv9"], AF.Identity, scale=T.kb[:, 11:12])
+        scan("vs", T.vs[:], T.keep[:, 0:256], T.zz[:, vv:vv + 256], ["keep", "zz"] + ["vv%d" % s for s in range(10)], ["vs"])
         ts("cs", T.zz[:, cs:cs + 256:16], T.vs[:, 15:256:16], 0.0, T.sm[:, 3:4], A.is_gt, A.mult, ["vs", "sig"], ["cs"])
-        scan("d03", T.d0[:, 3:1024:4], T.keep[:, 0:256], T.zz[:, cs:cs + 256], ["keep", "cs"], ["d03"])
-        scan("u", un[:], T.d0[:], ub[:], ["d01", "d02", "d03"] + ku, kn)
-        act("ut", T.ut[:], un[:].indirect(T.ltr[:]), kn + ["ltr"], ["ut"], AF.Identity, bias=-2.0 * LIFT)
-        scan("add", T["tb%d" % (h + 1)][:], un[:, 3:1024:4], T.ut[:], [kn[3], "ut"], ["tb%d" % (h + 1)], A.max)
+        scan("d03", T.d2[:, 1:512:2], T.keep[:, 0:256], T.zz[:, cs:cs + 256], ["keep", "cs"], ["d03"])
+        scan("u", un[:, 4:1540:3], T.d2[:], ub[:, 4:1540:3], ["d20", "d03", kb, ku], [kn, kbn])
+        act("ut", T.ut[:], un[:].indirect(T.ltr[:]), [kn, kbn, "ltr"], ["ut"], AF.Identity, bias=-2.0 * LIFT)
+        scan("add", T["tb%d" % (h + 1)][:], un[:, 7:1540:6], T.ut[:], [kn, "ut"], ["tb%d" % (h + 1)], A.max)
         lb = [6, 7, 0, 1]
+        nw = 160 if together else 64
+        for b in (0, 2, 1, 3):
+            mm(lb[b], max(nw, 128), T.wq[:, 128 * b:128 * b + 128], T.wp[:, 128 * b:128 * b + 128], qw[:, 0:max(nw, 128)], pw[:, 0:max(nw, 128)],
+               ["wq", "wp", "qe%d" % h, "arr%d" % h])
         for b in range(4):
-            mm(lb[b], 128, T.wq[:, 128 * b:128 * b + 128], T.wp[:, 128 * b:128 * b + 128], qw[:, 0:128], pw[:, 0:128], ["wq", "wp", "qe%d" % h, "arr%d" % h])
-        for b in range(4):
-            tt("wl%d" % b, T.wn[:, WN * b:WN * b + 64], bank(lb[b], 64), T.z32[:, b:256:4], A.add, ["z320"], ["wl%d" % b, "b%d" % lb[b]])
-        for b in range(4):
-            win = T.wn[:, WN * b:WN * b + WN].indirect(T.onew[:])
+            tt("wl%d" % b, T.wn[:, WN * b:WN * b + nw], bank(lb[b], nw), T.z32[:, b:4 * nw:4], A.add, ["z320"] + ["z321"] * together,
+               ["wl%d" % b, "b%d" % lb[b]] + ["we%d" % b] * together)
+        for nm, e, b, a, z in GATHERS:
+            win = T.wn[:, WN * b:WN * b + WN].indirect(T.onew[:, a:z])
             rd = ["wl%d" % b, "we%d" % b, "wg%d" % b, "onew"]
-            if b < 2:
-                act("xn%d" % b, T.xn[:, b:1024:4], win, rd, ["xn%d" % b], scale=0.03125)
+            if e == "a":
+                act(nm, T.xn[:, 64 * a + b:64 * z:4], win, rd, [nm], scale=0.03125)
             else:
-                ts("xn%d" % b, T.xn[:, b:1024:4], win, 0.03125, None, A.mult, None, rd, ["xn%d" % b])
+                ts(nm, T.xn[:, 64 * a + b:64 * z:4], win, 0.03125, None, A.mult, None, rd, [nm])
         nc, ns = T["xc%d" % (h + 1)], T["xs%d" % (h + 1)]
         for k in range(2):
             quant("q%d" % k, nc[:, 128 * k:128 * k + 128], ns[:, 128 * k:128 * k + 128], T.xn[:, 512 * k:512 * k + 512],
-                  four("xn"), ["xc%d%d" % (h + 1, k), "xs%d%d" % (h + 1, k)])
+                  [nm for nm, e, b, a, z in GATHERS if a < 8 * k + 8 and z > 8 * k], ["xc%d%d" % (h + 1, k), "xs%d%d" % (h + 1, k)])
     now[0] = R
     xc, xs = T["xc%d" % R], T["xs%d" % R]
     kx = [["xc%d%d" % (R, k), "xs%d%d" % (R, k)] for k in range(2)]
@@ -418,9 +471,9 @@ def rank_program(g, core, T, topo):
         cp("yo%d" % k, T.yo[:, 128 * k:128 * k + 128], bank(2 + k, 128), (), ["yo%d" % k, "b%d" % (2 + k)])
     dma(None, "s", T.oc[:], xc[:].bitcast(dt.uint8), kx[0] + kx[1], ["oc"])
     for k in range(4):
-        dma("os%d" % k, "s" if k < 2 else "a", T.osc[4 * k:4 * k + 4, :], xs[32 * k:32 * k + 4, :], kx[0] + kx[1], ["os%d" % k])
-    dma("y", "a", T.y[:], T.yo[:], ["yo0", "yo1"], ["y"])
-    dma(None, "s", T.ot[:], T.tb3[:], ["tb%d" % R], ["ot"])
-    op(None, "g", None, ["oc", "y", "ot"] + four("os"), ())
-    _emit(g, T, ops)
+        dma("os%d" % k if k > 1 else None, "s" if k < 2 else "a", T.osc[4 * k:4 * k + 4, :], xs[32 * k:32 * k + 4, :], kx[0] + kx[1], ["os%d" % k])
+    dma("y", "a", T.y[:], T.yo[:], ["yo0", "yo1"], ["y0", "y1"])
+    dma("ot", "a", T.ot[:], T.tb3[:], ["tb%d" % R], ["ot"])
+    op(None, "g", None, ["oc", "y0", "y1", "ot"] + four("os"), ())
+    _emit(g, T, ops, ["EVEN", "HASTE", "CATCH", "TAIL"] if late[0] else ["EVEN", "EVEN", "EVEN", "TAIL"])
     g.wait_ge(T.sem.sent, R * sum(len(topo.engines(core, c)) // 2 for c in to))

from concourse.mybir import dt, AluOpType, ActivationFunctionType

R = 3
F8, U8, BF, F32, I32, U16 = "float8_e4m3fn_x4", "uint8", "bfloat16", "float32", "int32", "uint16"
WN = 416
LIFT = 64.0

_SB = {
    BF: dict(xin=1024, uin=512, vin=512, ones=128, ident=128, ebig=528, yi=256, msk=256, keep=272, flip=240, targ=176, c16=256,
             cm=240, rk=256, nq=176, ob=176, lk=160, ms=160, hf=1024, aa=640, zl=512, ze=512, z32=640, wn=4 * WN, xn=1024,
             rs=512, sg=256, sh=4, zz=768, vs=256, d0=768, d2=512, sb=768, ub0=1552, ub1=1552, ut=256, tb0=256, tb1=256, tb2=256),
    F32: dict(pif=1, x2=48, x2s=48, x2t=48, tv=80, rkc=48, mb=240, sc=256, g1=240, sx=16, rr=64, of2=32, oft=32, rin=64, sm=8, kb=16, tw=192,
              tb3=256, yo=256),
    I32: dict(tin=256, ia=48, ib=48, ic=32, icol=16, ipart=2, ipm=4),
    U16: dict(lx=16, lu=16, lcmp=32, linv=16, ltr=16, lhalf=2, osec=16, oidx=16, othird=16, onew=16),
    F8: dict(wq=512, xq0=256, uq0=128, uq=128, vq=128, eq=512),
    U8: dict(wp=512, xp0=256, up0=128, up=128, vp=128, ep=512),
}
for _h in range(R):
    _SB[F8].update({"zq%d" % _h: 128, "qw%d" % _h: 192, "rc%d" % _h: 64})
    _SB[U8].update({"zp%d" % _h: 128, "pw%d" % _h: 192, "rp%d" % _h: 64})
for _h in range(R + 1):
    _SB[F8]["xc%d" % _h] = 256
    _SB[U8]["xs%d" % _h] = 256
SCRATCH = {_k: ("sbuf", [128, _n], _d) for _d in _SB for _k, _n in _SB[_d].items()}
SCRATCH["ps"] = ("psum", [128, 4096], F32)

SEMAPHORES = ["cv", "ca", "ct", "cg", "sent"] + ["arr%d" % h for h in range(R)] + ["dm%d" % k for k in range(20)]

GATHERS = [("xn0", "a", 0, 0, 16), ("xn1", "a", 1, 0, 16), ("xn5", "a", 3, 10, 16),
           ("xn2", "v", 2, 0, 8), ("xn3", "v", 3, 0, 10), ("xn6", "v", 2, 8, 16)]

LOWER = [("g1a", "a", 0, 4), ("g1v", "v", 4, 8), ("g1b", "a", 8, 15)]

A = AluOpType
AF = ActivationFunctionType

ORDER = {
    "EVEN": {
        "v": """ipm1 msk qx lhalf lcmp qu xc0 uc xc1 linv mb0 mb1 sc0 sc1 g1v tb0 cma cmb rka rkb vq add- nqE nqL obE obL ox0 ox1 ox2 ox3 osecE osecL
                lkE n0 sxL msE n1 sig othE rs0 zl0 zl1 zl2 zl3 sg rs1 qz
                kb0 rin2 oidxL rr0 tv1 lkL rho rr1 rin msL tv0 d10 othL tv2 rr2 ze0 ze1 ze2 rr3 ze3 of20 of21 qe onew z32e b3 we0 uinit oft we1 we2 vs we3
                wl0 onewT cs wl2 wl1 d03 wl3 xn2 *u xn3 xn6 q0 q1 u""",
        "a": """xs0 us xs1 g1a g1b hf0 wg0 hf1 hf2 t23 dab hf3 aE0 x2s aE1 aE2 wg1 aE3 aL0 x2t aL1 s64 sh aL2 d01
                A1 A2 aL3 B1 B2 A3 A4 z32l B3 B4 A5 A6 A0 tv3 B5 B6 A7 A8 e3 B7 B8 f3 e4 B0 f4 wg2 wg3 xn0 xn1 xn5 ut""",
    },
    "HASTE": {
        "v": """mb0 mb1 sc0 sc1 g1v add- cma cmb rka rkb nqE nqL obE sg obL ox0 ox1 ox2 ox3 sxL osecL osecE
                lkE oidxL n1 msE lkL othE n0 msL zl0 zl1 zl2 zl3 othL sig qz
                rs1 rs0 rr0 ze0 kb0 rin2 rr1 ze1 ze2 ze3 rin rr2 tv0 qe rr3 z32e vq onew rho
                wl0 d10 wl2 tv1 wl1 wl3 xn2 xn3 xn6 q0 tv2 q1 b3""",
        "a": """g1a g1b hf0 wg0 hf1 hf2 dab wg1 hf3 t23 aE0 sh aE1 aE2 x2t aE3 wg2 aL0 aL1 z32l aL2 s64 aL3
                A1 A2 d01 B1 B2 wg3 A3 A4 A0 B3 B4 A5 A6 xn0 xn1 xn5 B5 B6 A7 A8 tv3 B0 B7 B8 e3 e4 f3 f4""",
    },
    "CATCH": {
        "v": """mb0 mb1 sc0 sc1 g1v vs- cma cs- cmb d03- rka rkb u- nqE nqL obE sg rr0 obL osecE ox0 ox1 ox2 add- sig sxL osecL ox3 rr1 n1 tv0
                lkE n0 oidxL rs1 msE rs0 lkL tv1 othE rin2 kb0 rr2 msL zl0 rin zl1 zl2 zl3 othL rho tv2 qz
                rr3 ze0 ze1 ze2 of20 ze3 qe d10 z32e of21 b3 oft we0 we1 vs onewT we2 cs
                wl0 we3 wl2 d03 wl1 xn2 wl3 u xn3 xn6 q0 q1""",
        "a": """g1a g1b hf0 hf1 hf2 wg0 wg1 ut- dab t23 hf3 aE0 aE1 x2t aE2 aL0 aL1 sh s64 aE3 d01
                A1 A2 aL2 B1 B2 aL3 A3 A4 B3 B4 tv3 A0 A5 A6 B5 B6 wg2 A7 A8 e3 B7 B8 f3 e4 B0 f4 z32l wg3 xn0 xn1 xn5 ut""",
    },
    "TAIL": {"v": "add- yo0 yo1", "a": "os2 os3 ot y"},
}


def _mask(es):
    m = 0
    for e in es:
        m |= 1 << e
    return m


def _relays(src, dst, group, topo):
    cs = [c for c in topo.cores_of(src) if c not in group and topo.may_write(c, dst)]
    return sorted(cs, key=lambda c: (topo.die(c) != topo.die(src), c))[:2]


def _queues(ops, plan):
    at = {(o["h"], o["name"]): i for i, o in enumerate(ops) if o["name"]}
    qs = {}
    for e in ("v", "a", "t", "g", "s", None):
        if e not in ("v", "a"):
            qs[e] = [i for i, o in enumerate(ops) if o["e"] == e]
            continue
        qs[e] = [i for i, o in enumerate(ops) if o["e"] == e and not o["name"]]
        for h in range(R + 1):
            for w in ORDER[plan[h]][e].split():
                if w[0] == "*" and h != R - 1:
                    continue
                k = (h - 1, w[:-1]) if w.endswith("-") else (h, w.lstrip("*"))
                if k in at and at[k] not in qs[e]:
                    qs[e].append(at[k])
        assert sorted(qs[e]) == [i for i, o in enumerate(ops) if o["e"] == e]
    return qs


def _emit(g, T, ops, plan):
    q = {"v": g.vector, "a": g.scalar, "t": g.tensor, "g": g, "s": g.sync}
    cs = {"v": "cv", "a": "ca", "t": "ct", "g": "cg"}
    lastw, readers, deps = {}, {}, []
    for i, o in enumerate(ops):
        d = set(lastw[k] for k in o["r"] + o["w"] if k in lastw)
        for k in o["w"]:
            d.update(readers.get(k, []))
        deps.append(d)
        for k in o["r"]:
            readers.setdefault(k, []).append(i)
        for k in o["w"]:
            lastw[k] = i
            readers[k] = []
    qs = _queues(ops, plan)
    pos = {i: n for e in qs for n, i in enumerate(qs[e])}
    known = {e: ({}, set()) for e in q}
    snap = {i: ({}, set()) for i in qs[None]}
    waits, sig, nxt = {}, set(), {e: 0 for e in q}
    moved = True
    while moved:
        moved = False
        for e in q:
            while nxt[e] < len(qs[e]) and all(d in snap for d in deps[qs[e][nxt[e]]]):
                i = qs[e][nxt[e]]
                nxt[e] += 1
                moved = True
                kc, ks = known[e]
                waits[i] = []
                for d in sorted(deps[i], key=lambda d: -pos[d]):
                    p = ops[d]
                    if p["sem"] is None:
                        if kc.get(p["e"], -1) >= pos[d]:
                            continue
                        kc[p["e"]] = pos[d]
                    elif d in ks:
                        continue
                    else:
                        ks.add(d)
                    waits[i].append(d)
                    sig.add(d)
                    for k2, v2 in snap[d][0].items():
                        if kc.get(k2, -1) < v2:
                            kc[k2] = v2
                    ks.update(snap[d][1])
                snap[i] = (dict(kc), set(ks))
    assert all(nxt[e] == len(qs[e]) for e in q)
    val = {i: (o["sem"], o["n"]) for i, o in enumerate(ops) if o["sem"] is not None}
    for e in cs:
        for n, i in enumerate([i for i in qs[e] if ops[i]["sem"] is None and i in sig]):
            val[i] = (cs[e], n + 1)
    for e in q:
        for i in qs[e]:
            o = ops[i]
            for d in waits[i]:
                q[e].wait_ge(T.sem[val[d][0]], val[d][1])
            if o["f"] is None:
                continue
            ins = o["f"](q[e])
            if o["kind"] == "dma":
                ins.then_inc(T.sem[o["sem"]], 16)
            elif o["kind"] == "c" and i in sig:
                ins.then_inc(T.sem[val[i][0]], 1)


def _relay_program(g, core, T, topo, dst, part):
    rid, pid = topo.addr(dst, core)
    es = topo.engines(core, dst)
    n_in = len(topo.engines(core, core)) // 2
    for h in range(R):
        g.wait_ge(T.sem["arr%d" % h], n_in)
        if part == 0:
            o, i = T["qw%d" % h][:, 0:64].bitcast(dt.uint8), T["rc%d" % h][:].bitcast(dt.uint8)
        else:
            o, i = T["pw%d" % h][:, 0:64], T["rp%d" % h][:]
        g.remote_dma(o, i, T.sem["arr%d" % h], T.sem.sent, pid, rid, _mask(es))
    g.wait_ge(T.sem.sent, R * len(es))


def rank_program(g, core, T, topo):
    cores = list(T.cores)
    n = len(cores)
    rank = T.rank_of(core)
    if rank is None:
        for r in range(n):
            s, d = cores[r], cores[(r + 1) % n]
            if not topo.may_write(s, d):
                rl = _relays(s, d, cores, topo)
                if core in rl:
                    _relay_program(g, core, T, topo, d, rl.index(core))
        return
    nxt, prv = cores[(rank + 1) % n], cores[(rank - 1) % n]
    direct = topo.may_write(core, nxt)
    to = [nxt, nxt] if direct else _relays(core, nxt, cores, topo)
    if topo.may_write(prv, core):
        n_arr = len(topo.engines(prv, core))
    else:
        n_arr = sum(len(topo.engines(c, core)) for c in _relays(prv, core, cores, topo))

    late = [int((h % 2 == 0) != topo.may_write(prv, core)) for h in range(R)]

    ops = []
    ndma = [0]
    now = [0]

    def op(nm, e, f, r=(), w=(), kind="c", sem=None, cnt=0):
        ops.append({"name": nm, "h": now[0], "e": e, "f": f, "r": list(r), "w": list(w), "kind": kind, "sem": sem, "n": cnt})

    def dma(nm, e, out, in_, r=(), w=()):
        op(nm, e, lambda q: q.dma_start(out, in_), r, w, "dma", "dm%d" % ndma[0], 16)
        ndma[0] += 1

    def ts(nm, out, in0, s1, s2, o0, o1, r, w):
        if o1 is None:
            op(nm, "v", lambda q: q.tensor_scalar(out, in0, s1, None, o0), r, w)
        else:
            op(nm, "v", lambda q: q.tensor_scalar(out, in0, s1, s2, o0, o1), r, w)

    def tt(nm, out, a, b, o, r, w):
        op(nm, "v", lambda q: q.tensor_tensor(out, a, b, o), r, w)

    def scan(nm, out, a, b, r, w, o0=A.mult, first=0.0):
        op(nm, "v", lambda q: q.tensor_tensor_scan(out, a, b, first, o0, A.add), r, w)

    def cp(nm, out, a, r, w):
        op(nm, "v", lambda q: q.tensor_copy(out, a), r, w)

    def fill(ap, c, w):
        op(None, "v", lambda q: q.memset(ap, c), (), w)

    def act(nm, out, a, r, w, func=AF.Copy, **kw):
        op(nm, "a", lambda q: q.activation(out, a, func, **kw), r, w)

    def quant(nm, c, s, a, r, w):
        op(nm, "v", lambda q: q.quantize_mx(c, s, a), r, w)

    def mm(bank, n_, lc, ls, rc, rs_, r):
        op(None, "t", lambda q: q.matmul_mx(T.ps[:, 512 * bank:512 * bank + n_], lc, ls, rc, rs_, True, True), r, ["b%d" % bank])

    def iota(out, pat, base, cmul, w, flt=False):
        if flt:
            op(None, "g", lambda q: q.iota(out, pat, base, cmul, allow_small_or_imprecise_dtypes=True), (), w)
        else:
            op(None, "g", lambda q: q.iota(out, pat, base, cmul), (), w)

    def bank(b, n_):
        return T.ps[:, 512 * b:512 * b + n_]

    def four(name):
        return ["%s%d" % (name, b) for b in range(4)]

    u32 = dt.uint32
    vv, cs, rho = 0, 256, 512
    dma(None, "s", T.xin[:], T.x[:], (), ["xin"])
    dma(None, "s", T.uin[:], T.u[:], (), ["uin"])
    dma(None, "s", T.tin[:], T.tri[:], ["xin"], ["tin"])
    dma(None, "s", T.wq[:].bitcast(dt.uint8), T.wc[:], (), ["wq"])
    dma(None, "s", T.wp[:], T.ws[:], (), ["wp"])
    dma(None, "s", T.vin[:], T.v[:], (), ["vin"])
    fill(T.ones[:], 1.0, ["ones"])
    iota(T.icol[:], [[16, 16]], 0, 0, ["icol"])
    iota(T.ia[:, 0:16], [[1, 16]], 0, 16, ["ia0"])
    op(None, "g", lambda q: q.affine_select(T.ident[:], T.ones[:], [[-1, 128]], A.is_equal, 0.0, 0, 1), ["ones"], ["ident"])
    iota(T.ipart[:], [[0, 2]], 0, 1, ["ipart"])
    iota(T.ia[:, 16:32], [[16, 16]], 16, 16, ["ia1"])
    iota(T.ia[:, 32:48], [[0, 16]], 2303, -16, ["ia2"])
    iota(T.yi[:], [[0, 16], [1, 16]], 0, 0, ["yi"], True)
    iota(T.targ[:], [[1, 11], [-1, 16]], 1, 0, ["targ"], True)
    iota(T.rkc[:, 0:16], [[-1, 16]], 14, 0, ["rkc0"], True)
    iota(T.x2[:, 0:32], [[0, 2], [1, 16]], 0, 0, ["x2"], True)
    iota(T.x2[:, 32:48], [[33, 16]], -512, 0, ["inid"], True)
    iota(T.rkc[:, 16:32], [[1, 16]], 10, 0, ["rkc1"], True)
    iota(T.rkc[:, 32:48], [[-1, 16]], 16, 0, ["rkc2"], True)
    iota(T.ze[:, 384:512], [[0, 128]], 0, 0, ["zep"], True)
    iota(T.d0[:, 0:768:3], [[0, 256]], 0, 0, ["d00"], True)
    iota(T.d0[:, 2:768:3], [[0, 256]], -1, 0, ["d02"], True)
    iota(T.d2[:, 0:512:2], [[0, 256]], 0, 0, ["d20"], True)
    fill(T.zz[:, 0:256], 0.0, ["zz"])
    fill(T.ebig[:], 0.0, ["ebig"])
    for out, c, w in ((T.zz[:, cs:cs + 256], 0.0, "cs"), (T.zz[:, rho:rho + 256], 0.0, "rho"), (T.zl[:, 256:512], 0.0, "zlp"), (T.c16[:], 1.0 / 16.0, "c16")):
        act(None, out, T.zz[:, 0:256], ["zz"], [w], AF.Identity, bias=c)
    fill(T.keep[:], 1.0, ["keep"])
    fill(T.flip[:], 1.0, ["flip"])
    cp(None, T.lu[:], T.icol[:], ["icol"], ["lu"])
    ts(None, T.ib[:, 0:16], T.ia[:, 0:16], 255, None, A.bitwise_and, None, ["ia0"], ["ib0"])
    fill(T.keep[:, 0:272:16], 0.0, ["keep"])
    fill(T.flip[:, 0:240:16], 0.0, ["flip"])
    fill(T.sc[:, 255:256], -1.0e29, ["scp"])
    cp(None, T.lx[:], T.ib[:, 0:16], ["ib0"], ["lx"])
    cp(None, T.ebig[:, 3:515:4], T.ident[:], ["ident"], ["ebig"])
    fill(T.flip[:, 15:240:15], -1.0, ["flip"])
    ts(None, T.ipm[:, 0:2], T.ipart[:], 15, None, A.bitwise_and, None, ["ipart"], ["ipm0"])
    fill(T.rk[:, 255:256], 16.0, ["rkp"])
    ts(None, T.ltr[:], T.ib[:, 0:16], 6.0, 7.0, A.mult, A.add, ["ib0"], ["ltr"])
    for b in range(4):
        quant(None, T.eq[:, 128 * b:128 * b + 128], T.ep[:, 128 * b:128 * b + 128], T.ebig[:, 3 - b:515 - b], ["ebig"], ["e%d" % b])
        if b == 1:
            ts(None, T.ib[:, 16:48], T.ia[:, 16:48], 255, None, A.bitwise_and, None, ["ia1", "ia2"], ["ib1"])
    cp(None, T.pif[:], T.ipm[:, 0:1], ["ipm0"], ["pif"])
    tt(None, T.ic[:, 0:16], T.ib[:, 16:32], T.icol[:], A.min, ["ib1", "icol"], ["ic0"])
    tt(None, T.ic[:, 16:32], T.ib[:, 16:32], T.icol[:], A.max, ["ib1", "icol"], ["ic1"])
    cp("linv", T.linv[:], T.ib[:, 32:48], ["ib1"], ["linv"])
    ts("ipm1", T.ipm[:, 2:4], T.ipart[:], 31, None, A.bitwise_and, None, ["ipart"], ["ipm1"])
    ts("msk", T.msk[:], T.yi[:], T.pif[:], None, A.is_equal, None, ["yi", "pif"], ["msk"])
    ts("lcmp", T.lcmp[:], T.ic[:], 15.0, None, A.add, None, ["ic0", "ic1"], ["lcmp"])
    cp("lhalf", T.lhalf[:], T.ipm[:, 2:4], ["ipm1"], ["lhalf"])
    quant("qx", T.xq0[:], T.xp0[:], T.xin[:], ["xin"], ["xq0"])
    quant("qu", T.uq0[:], T.up0[:], T.uin[:], ["uin"], ["uq0"])
    for k in range(2):
        cp("xc%d" % k, T.xc0[:, 128 * k:128 * k + 128].bitcast(u32), T.xq0[:].bitcast(u32).indirect(T.lx[:, 8 * k:8 * k + 8]), ["xq0", "lx"], ["xc0%d" % k])
        act("xs%d" % k, T.xs0[:, 128 * k:128 * k + 128], T.xp0[:].indirect(T.lx[:, 8 * k:8 * k + 8]), ["xq0", "lx"], ["xs0%d" % k])
    cp("uc", T.uq[:].bitcast(u32), T.uq0[:].bitcast(u32).indirect(T.lu[:, 0:8]), ["uq0", "lu"], ["uq"])
    act("us", T.up[:], T.up0[:].indirect(T.lu[:, 0:8]), ["uq0", "lu"], ["up"])
    act("x2s", T.x2s[:], T.x2[:], ["x2", "inid"], ["x2s"], scale=1.0 / 512.0)

    def o_(j):
        return T.ob[:, 16 * j + 15:16 * j + 16]

    def plane(b):
        return T.hf[:, 256 * b:256 * b + 256]

    for h in range(R):
        now[0] = h
        xc, xs = T["xc%d" % h], T["xs%d" % h]
        kx = [["xc%d%d" % (h, k), "xs%d%d" % (h, k)] for k in range(2)]
        tb, ktb = T["tb%d" % h], "tb%d" % h
        ub, un = T["ub%d" % (h % 2)], T["ub%d" % (1 - h % 2)]
        ku, kn, kb, kbn = "u%d" % (h % 2), "u%d" % (1 - h % 2), "bb%d" % (h % 2), "bb%d" % (1 - h % 2)
        zq, zp, qw, pw = T["zq%d" % h], T["zp%d" % h], T["qw%d" % h], T["pw%d" % h]
        if h == 0:
            cp("tb0", T.tb0[:], T.tin[:], ["tin"], ["tb0"])
            ts("uinit", ub[:, 7:1540:6], T.tb0[:], 0.5, LIFT, A.mult, A.add, ["tb0"], [ku])
        for k in range(2):
            mm(k, 128, T.uq[:], T.up[:], xc[:, 128 * k:128 * k + 128], xs[:, 128 * k:128 * k + 128], ["uq", "up"] + kx[k])
        for b in range(4):
            mm(2 + b, 256, T.eq[:, 128 * b:128 * b + 128], T.ep[:, 128 * b:128 * b + 128], xc[:], xs[:], ["e%d" % b] + kx[0] + kx[1])
        halves = [(0, 128), (128, 240)]
        for k, (a, z) in enumerate(halves):
            tt("mb%d" % k, T.mb[:, a:z], bank(k, z - a), T.msk[:, a:z], A.mult, ["msk"], ["mb%d" % k, "b%d" % k])
            scan("sc%d" % k, T.sc[:, a:z], T.keep[:, a:z], T.mb[:, a:z], ["keep", "mb%d" % k], ["sc%d" % k])
        for b in range(4):
            act("hf%d" % b, plane(b), bank(2 + b, 256), (), ["hf%d" % b, "b%d" % (2 + b)], scale=0.5)
            act("wg%d" % b, T.wn[:, WN * b + 160:WN * b + WN], plane(b), ["hf%d" % b], ["wg%d" % b], scale=64.0)
        for nm, e, a, z in LOWER:
            (act if e == "a" else cp)(nm, T.g1[:, 16 * a:16 * z], T.sc[:, 0:128 if a < 8 else 240].indirect(T.lcmp[:, a:z]), ["sc0", "lcmp"] + ["sc1"] * (a // 8), [nm])
        for k, (a, z) in enumerate(halves):
            c = "ab"[k]
            tt("cm" + c, T.cm[:, a:z], T.sc[:].indirect(T.lcmp[:, 16 + a // 16:16 + z // 16]), T.g1[:, a:z], A.is_le,
               ["sc0", "sc1", "scp", "lcmp"] + [nm for nm, e, a1, z1 in LOWER if a1 // 8 == k], ["cm" + c])
            scan("rk" + c, T.rk[:, a:z], T.flip[:, a:z], T.cm[:, a:z], ["flip", "cm" + c], ["rk" + c])
        krk = ["rka", "rkb", "rkp"]
        for c, a, z, s0, s1 in (("E", 0, 5, 0, 4), ("L", 5, 11, 4, 10)):
            tt("nq" + c, T.nq[:, 16 * a:16 * z], T.rk[:].indirect(T.linv[:, 0:z - a]), T.targ[:, 16 * a:16 * z], A.not_equal, krk + ["linv", "targ"], ["nq" + c])
            scan("ob" + c, T.ob[:, 16 * a:16 * z], T.nq[:, 16 * a:16 * z], T.keep[:, 16 * a + 1:16 * z + 1], ["nq" + c, "keep"], ["ob" + c])
            if c == "E":
                for j in range(4):
                    ts("ox%d" % j, T.oidx[:, j:j + 1], o_(j), 16.0, o_(j + 1), A.mult, A.add, ["obE"], ["oidxE%d" % j])
            else:
                scan("sxL", T.sx[:, 0:7], T.c16[:, 0:7], T.ob[:, 79:176:16], ["c16", "obE", "obL"], ["sxL"])
                ts("oidxL", T.oidx[:, 4:10], T.sx[:, 1:7], 16.0, -0.47, A.mult, A.add, ["sxL"], ["oidxL"])
            ts("osec" + c, T.osec[:, s0:s1], T.ob[:, 16 * s0 + 31:16 * s1 + 16:16], 16.0, T.pif[:], A.mult, A.add, ["ob" + c, "pif"], ["osec" + c])
            tt("lk" + c, T.lk[:, 16 * s0:16 * s1], tb[:].indirect(T.oidx[:, s0:s1]), T.msk[:, 16 * s0:16 * s1], A.mult,
               [ktb, "msk"] + (four("oidxE") if c == "E" else ["oidxL"]), ["lk" + c])
            scan("ms" + c, T.ms[:, 16 * s0:16 * s1], T.keep[:, 16 * s0:16 * s1], T.lk[:, 16 * s0:16 * s1], ["keep", "lk" + c], ["ms" + c])
            ts("oth" + c, T.othird[:, s0:s1], T.ms[:, 16 * s0 + 15:16 * s1:16], 16.0, T.pif[:], A.mult, A.add, ["ms" + c, "pif"], ["oth" + c])
            for b in range(4):
                act("a%s%d" % (c, b), T.aa[:, 160 * b + 16 * s0:160 * b + 16 * s1], plane(b).indirect(T.osec[:, s0:s1]), ["hf%d" % b, "osec" + c], ["a%s%d" % (c, b)])
        tt("rr0", T.rr[:, 0:16], T.rk[:, 15:256:16], T.rkc[:, 0:16], A.add, krk + ["rkc0"], ["rr0"])
        ts("rr1", T.rr[:, 16:32], T.rr[:, 0:16], -9.0, 30.0, A.add, A.mult, ["rr0"], ["rr1"])
        tt("rr2", T.rr[:, 32:48], T.rr[:, 0:16], T.rr[:, 16:32], A.max, ["rr0", "rr1"], ["rr2"])
        tt("rr3", T.rr[:, 48:64], T.rr[:, 32:48], T.rkc[:, 16:32], A.min, ["rr2", "rkc1"], ["rr"])
        if h < R - 1:
            ts("onew", T.onew[:], T.rr[:, 48:64], 16.0, T.pif[:], A.mult, A.add, ["rr", "pif"], ["onew"])
        else:
            for k in range(2):
                ts("of2%d" % k, T.of2[:, 16 * k:16 * k + 16], T.rr[:, 48:64], 16.0, T.pif[:], A.mult, A.add, ["rr", "pif"], ["of2%d" % k])
            op("oft", "v", lambda q: q.transpose(T.oft[:], T.of2[:]), ["of20", "of21"], ["oft"])
            cp("onewT", T.onew[:], T.oft[:].indirect(T.lhalf[:, 0:1]), ["oft", "lhalf"], ["onew"])
        for b in range(4):
            tt("zl%d" % b, T.zl[:, b:256:4], plane(b).indirect(T.othird[:, 0:4]), T.aa[:, 160 * b:160 * b + 64], A.add,
               ["hf%d" % b, "othE", "aE%d" % b], ["zl%d" % b])
        quant("qz", zq[:], zp[:], T.zl[:], four("zl") + ["zlp"], ["zq%d" % h])
        for part in range(2):
            rid, pid = topo.addr(to[part], core)
            es = topo.engines(core, to[part])
            es = es[part::2]
            if part == 0:
                src = zq[:, 0:64].bitcast(dt.uint8)
                dst = (qw[:, 0:64] if direct else T["rc%d" % h][:]).bitcast(dt.uint8)
            else:
                src = zp[:, 0:64]
                dst = pw[:, 0:64] if direct else T["rp%d" % h][:]
            op(None, "g", lambda q, dst=dst, src=src, pid=pid, rid=rid, m=_mask(es), s=T.sem["arr%d" % h]: q.remote_dma(dst, src, s, T.sem.sent, pid, rid, m),
               ["zq%d" % h], (), "remote")
        op(None, None, None, (), ["arr%d" % h], "ext", "arr%d" % h, n_arr)
        act("z32l", T.z32[:, 0:256], T.zl[:, 0:256], four("zl"), ["z320"], scale=32.0)
        for b in range(4):
            tt("ze%d" % b, T.ze[:, b:384:4], plane(b).indirect(T.othird[:, 4:10]), T.aa[:, 160 * b + 64:160 * b + 160], A.add,
               ["hf%d" % b, "othL", "aL%d" % b], ["ze%d" % b])
        quant("qe", qw[:, 64:192], pw[:, 64:192], T.ze[:], four("ze") + ["zep"], ["qe%d" % h])
        together = 1 - late[h]
        for b in range(0 if together else 4):
            mm(2 + b, 128, T.wq[:, 128 * b:128 * b + 128], T.wp[:, 128 * b:128 * b + 128], qw[:, 64:192], pw[:, 64:192], ["wq", "wp", "qe%d" % h])
        ts("z32e", T.z32[:, 256:640], T.ze[:, 0:384], 32.0, None, A.mult, None, four("ze"), ["z321"])
        for b in range(0 if together else 4):
            tt("we%d" % b, T.wn[:, WN * b + 64:WN * b + 160], bank(2 + b, 96), T.z32[:, 256 + b:640:4], A.add, ["z321"], ["we%d" % b, "b%d" % (2 + b)])
        if h == 1:
            quant("vq", T.vq[:], T.vp[:], T.vin[:], ["vin"], ["vq"])
        tt("sg", T.sg[:, 15:256:16], T.nq[:, 0:16], T.nq[:, 16:32], A.subtract, ["nqE"], ["sg"])
        ts("sig", T.sm[:, 3:4], o_(1), o_(0), 0.5, A.is_gt, A.subtract, ["obE"], ["sig"])
        act("dab", T.sh[:, 1:2], o_(0), ["obE"], ["dab"], AF.Abs, scale=-1.0, bias=o_(1))
        act("s64", T.sm[:, 5:6], T.sm[:, 3:4], ["sig"], ["s64"], scale=64.0)
        for k in range(2):
            ts("n%d" % k, T.sb[:, 1 + k:768:3], tb[:], o_(k), T.sh[:, 1:2], A.not_equal, A.mult, [ktb, "obE", "dab"], ["sb%d" % k])
            scan("rs%d" % k, T.rs[:, 256 * k:256 * k + 256], T.sb[:, 1 + k:768:3], T.c16[:], ["sb%d" % k, "c16"], ["rs%d" % k], A.min)
        tt("rin", T.rin[:, 0:32], T.x2s[:, 0:32], T.rs[:, 15:512:16], A.subtract, ["rs0", "rs1", "x2s"], ["rin"])
        tt("rho", T.zz[:, rho:rho + 256:16], T.rs[:, 15:256:16], T.rs[:, 271:512:16], A.subtract, ["rs0", "rs1"], ["rho"])
        scan("d10", T.sb[:, 0:768:3], T.keep[:, 0:256], T.zz[:, rho:rho + 256], ["keep", "rho"], ["sb2"])
        act("d01", T.d0[:, 1:768:3], T.sg[:].indirect(T.linv[:, 0:16]), ["sg", "linv", "s64"], ["d01"], scale=T.sm[:, 5:6])
        scan("b3", ub[:, 0:1536:2], T.d0[:], T.sb[:], ["d00", "d01", "d02", "sb0", "sb1", "sb2"], [kb])
        act("t23", T.sm[:, 0:2], T.ob[:, 47:64:16], ["obE"], ["t23"], AF.Identity, scale=-1.0 / 16.0, bias=1.0)
        act("sh", T.sh[:, 0:1], T.sm[:, 0:1], ["t23"], ["sh"], AF.Identity, scale=-1.0, bias=T.sm[:, 1:2])
        act("x2t", T.x2t[:], T.x2s[:], ["t23", "x2s"], ["x2t"], AF.Identity, bias=T.sm[:, 0:1])
        tt("rin2", T.rin[:, 32:64], T.x2t[:, 0:32], T.rs[:, 15:512:16], A.subtract, ["rs0", "rs1", "x2t"], ["rin2"])
        ts("kb0", T.kb[:, 0:1], T.ms[:, 15:16], o_(2), T.sh[:, 0:1], A.is_equal, A.mult, ["msE", "obE", "sh"], ["kb0"])
        tt("tv0", T.tv[:, 0:16], T.rr[:, 0:16], T.rkc[:, 32:48], A.min, ["rr0", "rkc2"], ["tv0"])
        ts("tv1", T.tv[:, 16:32], T.yi[:, 0:16], T.ms[:, 15:16], 16.0, A.not_equal, A.mult, ["yi", "msE"], ["tv1"])
        tt("tv2", T.tv[:, 32:48], T.tv[:, 0:16], T.tv[:, 16:32], A.min, ["tv0", "tv1"], ["tv2"])
        act("tv3", T.tv[:, 48:64], T.tv[:, 32:48], ["tv2"], ["tv3"], AF.Relu, bias=-1.0)
        steps = [(0, None)] + [(max(s - 2, 0), ((s + 1) // 2 + s) % 2) for s in range(1, 9)]
        for s, (fr, row) in enumerate(steps):
            if row is None:
                src, ks = T.x2t[:, 32:48], "x2t"
            else:
                src, ks = (T.rin[:, 16 * row:16 * row + 16], "rin") if fr else (T.rin[:, 32 + 16 * row:48 + 16 * row], "rin2")
            act("A%d" % s, T.tw[:, 16 * s:16 * s + 16], src, [ks, "kb%d" % fr], ["tw%d" % s], AF.Abs, bias=T.kb[:, fr:fr + 1])
            kw = {"accum_out": T.kb[:, s:s + 1]} if 0 < s < 10 else {}
            act("B%d" % s, T.zz[:, vv + s:vv + 256:16], T.tw[:, 16 * s:16 * s + 16], ["tw%d" % s, "zz"], ["vv%d" % s] + (["kb%d" % s] if kw else []),
                AF.Relu, bias=1.0, scale=-32.0, **kw)
        act("e3", T.kb[:, 10:11], T.kb[:, 5:6], ["kb5", "kb6"], ["e3"], AF.Abs, scale=-1.0, bias=T.kb[:, 6:7])
        act("f3", T.tv[:, 64:80], T.tv[:, 48:64], ["tv3", "e3"], ["f3"], AF.Identity, scale=T.kb[:, 10:11])
        act("e4", T.kb[:, 11:12], T.kb[:, 7:8], ["kb7", "kb8"], ["e4"], AF.Abs, scale=-1.0, bias=T.kb[:, 8:9])
        act("f4", T.zz[:, vv + 9:vv + 256:16], T.tv[:, 64:80], ["f3", "e4", "zz"], ["vv9"], AF.Identity, scale=T.kb[:, 11:12])
        scan("vs", T.vs[:], T.keep[:, 0:256], T.zz[:, vv:vv + 256], ["keep", "zz"] + ["vv%d" % s for s in range(10)], ["vs"])
        ts("cs", T.zz[:, cs:cs + 256:16], T.vs[:, 15:256:16], 0.0, T.sm[:, 3:4], A.is_gt, A.mult, ["vs", "sig"], ["cs"])
        scan("d03", T.d2[:, 1:512:2], T.keep[:, 0:256], T.zz[:, cs:cs + 256], ["keep", "cs"], ["d03"])
        scan("u", un[:, 4:1540:3], T.d2[:], ub[:, 4:1540:3], ["d20", "d03", kb, ku], [kn, kbn])
        act("ut", T.ut[:], un[:].indirect(T.ltr[:]), [kn, kbn, "ltr"], ["ut"], AF.Identity, bias=-2.0 * LIFT)
        scan("add", T["tb%d" % (h + 1)][:], un[:, 7:1540:6], T.ut[:], [kn, "ut"], ["tb%d" % (h + 1)], A.max)
        lb = [6, 7, 0, 1]
        nw = 160 if together else 64
        for b in (0, 2, 1, 3):
            mm(lb[b], max(nw, 128), T.wq[:, 128 * b:128 * b + 128], T.wp[:, 128 * b:128 * b + 128], qw[:, 0:max(nw, 128)], pw[:, 0:max(nw, 128)],
               ["wq", "wp", "qe%d" % h, "arr%d" % h])
        for b in range(4):
            tt("wl%d" % b, T.wn[:, WN * b:WN * b + nw], bank(lb[b], nw), T.z32[:, b:4 * nw:4], A.add, ["z320"] + ["z321"] * together,
               ["wl%d" % b, "b%d" % lb[b]] + ["we%d" % b] * together)
        for nm, e, b, a, z in GATHERS:
            win = T.wn[:, WN * b:WN * b + WN].indirect(T.onew[:, a:z])
            rd = ["wl%d" % b, "we%d" % b, "wg%d" % b, "onew"]
            if e == "a":
                act(nm, T.xn[:, 64 * a + b:64 * z:4], win, rd, [nm], scale=0.03125)
            else:
                ts(nm, T.xn[:, 64 * a + b:64 * z:4], win, 0.03125, None, A.mult, None, rd, [nm])
        nc, ns = T["xc%d" % (h + 1)], T["xs%d" % (h + 1)]
        for k in range(2):
            quant("q%d" % k, nc[:, 128 * k:128 * k + 128], ns[:, 128 * k:128 * k + 128], T.xn[:, 512 * k:512 * k + 512],
                  [nm for nm, e, b, a, z in GATHERS if a < 8 * k + 8 and z > 8 * k], ["xc%d%d" % (h + 1, k), "xs%d%d" % (h + 1, k)])
    now[0] = R
    xc, xs = T["xc%d" % R], T["xs%d" % R]
    kx = [["xc%d%d" % (R, k), "xs%d%d" % (R, k)] for k in range(2)]
    for k in range(2):
        mm(2 + k, 128, T.vq[:], T.vp[:], xc[:, 128 * k:128 * k + 128], xs[:, 128 * k:128 * k + 128], ["vq"] + kx[k])
        cp("yo%d" % k, T.yo[:, 128 * k:128 * k + 128], bank(2 + k, 128), (), ["yo%d" % k, "b%d" % (2 + k)])
    dma(None, "s", T.oc[:], xc[:].bitcast(dt.uint8), kx[0] + kx[1], ["oc"])
    for k in range(4):
        dma("os%d" % k if k > 1 else None, "s" if k < 2 else "a", T.osc[4 * k:4 * k + 4, :], xs[32 * k:32 * k + 4, :], kx[0] + kx[1], ["os%d" % k])
    dma("y", "a", T.y[:], T.yo[:], ["yo0", "yo1"], ["y0", "y1"])
    dma("ot", "a", T.ot[:], T.tb3[:], ["tb%d" % R], ["ot"])
    op(None, "g", None, ["oc", "y0", "y1", "ot"] + four("os"), ())
    _emit(g, T, ops, ["EVEN", "HASTE", "CATCH", "TAIL"] if late[0] else ["EVEN", "EVEN", "EVEN", "TAIL"])
    g.wait_ge(T.sem.sent, R * sum(len(topo.engines(core, c)) // 2 for c in to))
